import numpy as np
import ml_dtypes


def mxq(x, axis, fmt="e4m3"):
    dtype, down = {"e4m3": (ml_dtypes.float8_e4m3fn, 7), "e5m2": (ml_dtypes.float8_e5m2, 14)}[fmt]
    v = np.moveaxis(np.asarray(x, np.float32).astype(ml_dtypes.bfloat16).astype(np.float64), axis, -1)
    blocks = v.reshape(v.shape[:-1] + (-1, 32))
    amax = np.abs(blocks).max(-1, keepdims=True)
    byte = np.maximum(np.where(amax > 0, np.frexp(amax)[1] - 1 + 127, 0) - down, 1)
    scale = np.exp2(byte - 127.0)
    codes = (blocks / scale).astype(np.float32).astype(dtype).astype(np.float64)
    return np.moveaxis((codes * scale).reshape(v.shape), -1, axis)


WIDE = False


def mx_kscale(k):
    if not WIDE:
        return np.ones(k)
    levels = np.array([10, -10, 5, -5, 0])
    if k % 512:
        return np.exp2(np.random.permutation(np.resize(levels, k // 32))).repeat(32)
    a = np.empty((k // 512, 16))
    for p in range(k // 512):
        a[p, :8] = np.random.permutation(np.resize(levels, 8))
        for g in range(8):
            far = levels[np.abs(levels - a[p, g]) >= 10]
            a[p, g + 8] = far[np.random.randint(len(far))]
    return np.exp2(a.ravel()).repeat(32)


def f64(x):
    return np.asarray(x).astype(np.float64)


def striped8(idx):
    return np.concatenate([x.reshape(-1, 16).T for x in idx]).astype(np.uint16)


def runs(offs, k):
    lists = np.stack([offs[16 * r : 16 * r + 16].T.reshape(-1) for r in range(8)]).astype(np.int64)
    return lists[np.arange(k) % 512 // 64]


def pack_weight(w):
    k, n = w.shape
    w = f64(np.asarray(w, np.float32).astype(ml_dtypes.bfloat16)).reshape(k // 32, 32, n)
    amax = np.abs(w).max(1)
    byte = np.clip(np.where(amax > 0, np.frexp(amax)[1] - 1 + 127 - 7, 1), 1, 254)
    scaled = (w * np.exp2(127.0 - byte)[:, None, :]).reshape(k, n).astype(np.float32)
    words = np.ascontiguousarray(scaled.reshape(k // 512, 128, 4, n).transpose(0, 1, 3, 2)).astype(ml_dtypes.float8_e4m3fn).view(np.uint8)
    return words, np.ascontiguousarray(byte.astype(np.uint8).reshape(k // 512, 16, n))


def unpack_weight(words, scales):
    g, p, n, _ = words.shape
    vals = np.ascontiguousarray(words).view(ml_dtypes.float8_e4m3fn).astype(np.float64) * np.repeat(np.exp2(scales.astype(np.float64) - 127.0), 8, axis=1)[..., None]
    return vals.transpose(0, 1, 3, 2).reshape(g * 512, n)


E2M1 = np.array([0.0, 0.5, 1.0, 1.5, 2.0, 3.0, 4.0, 6.0, -0.0, -0.5, -1.0, -1.5, -2.0, -3.0, -4.0, -6.0])


def pack_fp4(w):
    k, n = w.shape
    w = f64(np.asarray(w, np.float32).astype(ml_dtypes.bfloat16)).reshape(k // 32, 32, n)
    amax = np.abs(w).max(1)
    mant, ex = np.frexp(amax / 6.0)
    byte = np.clip(np.where(amax > 0, np.where(mant > 0.5, ex, ex - 1) + 127, 1), 1, 254)
    scaled = (w * np.exp2(127.0 - byte)[:, None, :]).reshape(k, n).astype(np.float32)
    c = np.ascontiguousarray(scaled.reshape(k // 512, 128, 4, n).transpose(0, 1, 3, 2)).astype(ml_dtypes.float4_e2m1fn).view(np.uint8) & 0xF
    words = (c[..., 0::2] | (c[..., 1::2] << 4)).reshape(k // 512, 128, 2 * n)
    return np.ascontiguousarray(words), np.ascontiguousarray(byte.astype(np.uint8).reshape(k // 512, 16, n))


def unpack_fp4(words, scales):
    g, _, n = scales.shape
    words = np.ascontiguousarray(words).reshape(g, 128, n, 2)
    nib = np.empty((g, 128, n, 4), np.uint8)
    nib[..., 0::2] = words & 0xF
    nib[..., 1::2] = words >> 4
    vals = E2M1[nib] * np.repeat(np.exp2(scales.astype(np.float64) - 127.0), 8, axis=1)[..., None]
    return vals.transpose(0, 1, 3, 2).reshape(g * 512, n)


def gelu(v):
    return 0.5 * v * (1.0 + np.tanh(np.sqrt(2.0 / np.pi) * (v + 0.044715 * v**3)))


K, T, S, H, N = 1024, 2048, 1024, 512, 128


def setup_inputs():
    n = np.random.standard_normal
    s = mx_kscale(K)[:, None]
    u = mx_kscale(H)
    packed_xT = pack_weight(n((K, T)) * s)
    packed_w2 = pack_fp4(n((H, N)) / np.sqrt(H) / u[:, None])
    return {
        "x_words": packed_xT[0],
        "x_scales": packed_xT[1],
        "w1": (n((K, H)) / np.sqrt(K) / s * u).astype(np.float32),
        "w2_words": packed_w2[0],
        "w2_scales": packed_w2[1],
        "pos": (0.5 * n((H, S)) * u[:, None]).astype(np.float32),
        "offs": striped8(np.random.randint(0, T, (8, S))),
    }


def reference(x_words, x_scales, w1, w2_words, w2_scales, pos, offs):
    xq = unpack_weight(x_words, x_scales)[np.arange(K)[:, None], runs(offs, K)]
    h = gelu((mxq(f64(w1), 0, "e4m3").T @ xq) + f64(pos))
    return unpack_fp4(w2_words, w2_scales).T @ mxq(h, 0, "e4m3")

@@ -1,0 +1,165 @@
+from contextlib import ExitStack
+
+import concourse.mybir as mybir
+
+K, T, S, H, N = 1024, 2048, 1024, 512, 128
+FLOPS = 2 * K * H * S + 2 * H * N * S
+
+F32 = mybir.dt.float32
+BF16 = mybir.dt.bfloat16
+I32 = mybir.dt.int32
+U32 = mybir.dt.uint32
+U16 = mybir.dt.uint16
+U8 = mybir.dt.uint8
+FP8X4 = mybir.dt.float8_e4m3fn_x4
+FP4X4 = mybir.dt.float4_e2m1fn_x4
+GELU = mybir.ActivationFunctionType.Gelu_apprx_tanh
+ADD = mybir.AluOpType.add
+
+P = 128
+PACK = 4
+PASSES = K // (P * PACK)
+HALF = 512
+POS_W = 256
+CHUNKS = (128, 128, 256, 256, 128, 128)
+SCALAR_M = (64, 48)
+
+
+def tile_picked_phpq_gelu_p_kernel(tc, x_words, x_scales, w1, w2_words, w2_scales, pos, offs, out):
+    nc = tc.nc
+    with ExitStack() as ctx:
+        keep = ctx.enter_context(tc.tile_pool(name="keep", bufs=1))
+        ring = ctx.enter_context(tc.tile_pool(name="ring", bufs=3))
+        psum = ctx.enter_context(tc.psum_pool(name="psum", bufs=1))
+
+        lists = keep.tile([P, S // 16], U16, name="lists")
+        nc.sync.dma_start(lists[:], offs)
+
+        scale_table = keep.tile([P, T], U8, name="scale_table", tag="early_a", align_bytes=64)
+        nc.vector.memset(scale_table[:].bitcast(I32), 0)
+        for z in range(PASSES):
+            rows = x_scales[z].rearrange("(g s) c -> s g c", s=2)
+            for s in range(2):
+                nc.sync.dma_start(scale_table[4 * z + s : P : 16, :].bitcast(I32), rows[s].bitcast(I32))
+
+        warm = keep.tile([P, 2], F32, name="warm")
+        nc.vector.memset(warm[:, 0:1], 0.0)
+        nc.scalar.activation(warm[:, 1:2], warm[:, 0:1], GELU)
+
+        w2_codes = keep.tile([P, 2 * N], U8, name="w2_codes", align_bytes=64)
+        w2_plane = keep.tile([P, N], U8, name="w2_plane", align_bytes=64)
+        nc.gpsimd.memset(w2_plane[:].bitcast(I32), 0)
+        nc.gpsimd.dma_start(w2_codes[:].bitcast(I32), w2_words[0].bitcast(I32))
+        for q in range(4):
+            nc.gpsimd.dma_start(w2_plane[32 * q : 32 * q + 4, :].bitcast(I32), w2_scales[0, 4 * q : 4 * q + 4, :].bitcast(I32))
+
+        word_table, w1_raw = [], []
+        for z in range(PASSES):
+            table = keep.tile([P, T], I32, name=f"word_table{z}", align_bytes=64)
+            nc.sync.dma_start(table[:], x_words[z].rearrange("p c r -> p (c r)").bitcast(I32))
+            word_table.append(table)
+            if z == 0:
+                raw = keep.tile([P, PACK, H], F32, name="w1_raw0")
+                nc.sync.dma_start(raw[:], w1[:512, :].rearrange("(p j) c -> p j c", j=PACK))
+                w1_raw.append(raw)
+
+        picked_scales = keep.tile([P, S], U8, name="picked_scales", tag="early_b", align_bytes=64)
+        nc.vector.tensor_copy(picked_scales[:], scale_table[:].indirect(lists[:]))
+        x_plane = keep.tile([P, S], U8, name="x_plane", align_bytes=64)
+        nc.vector.tensor_copy(x_plane[:].bitcast(I32), picked_scales[:].bitcast(I32))
+        for z in range(PASSES):
+            for s in range(2):
+                nc.scalar.dma_start(
+                    x_plane[4 * z + 2 + s : P : 32, :].bitcast(I32),
+                    picked_scales[16 + 4 * z + s : P : 32, :].bitcast(I32),
+                )
+
+        raw = keep.tile([P, PACK, H], F32, name="w1_raw1", tag="early_a", align_bytes=64)
+        nc.sync.dma_start(raw[:], w1[512:, :].rearrange("(p j) c -> p j c", j=PACK))
+        w1_raw.append(raw)
+
+        pos_sb = keep.tile([P, S // POS_W, PACK, POS_W], F32, name="pos_sb", tag="early_b", align_bytes=64)
+        pos_rows = pos.rearrange("(p t) c -> p t c", t=PACK)
+        for c in range(S // POS_W):
+            nc.sync.dma_start(pos_sb[:, c], pos_rows[:, :, c * POS_W : (c + 1) * POS_W])
+
+        banks = [[psum.tile([P, HALF], F32, name=f"bank{h}{t}", tag=f"bank{h}{t}") for t in range(PACK)] for h in range(2)]
+        for z in range(PASSES):
+            picked = []
+            for h in range(2):
+                words = keep.tile([P, HALF], U32, name=f"picked{z}{h}", align_bytes=64)
+                nc.vector.tensor_copy(words[:], word_table[z][:].bitcast(U32).indirect(lists[:, 32 * h : 32 * (h + 1)]))
+                picked.append(words)
+            grouped = keep.tile([P, PACK * H], BF16, name=f"w1_grouped{z}", align_bytes=64)
+            dst = grouped[:].rearrange("p (t m j) -> p m j t", t=PACK, j=PACK)
+            src = w1_raw[z][:].rearrange("p j (m t) -> p m j t", t=PACK)
+            m_split = SCALAR_M[z]
+            nc.scalar.copy(dst[:, :m_split], src[:, :m_split])
+            nc.vector.tensor_copy(dst[:, m_split:], src[:, m_split:])
+            w1_codes = keep.tile([P, H], U32, name=f"w1_codes{z}", align_bytes=64)
+            w1_plane = keep.tile([P, H], U8, name=f"w1_plane{z}", align_bytes=64)
+            for t in range(PACK):
+                nc.vector.quantize_mx(
+                    out=w1_codes[:, t * P : (t + 1) * P].bitcast(FP8X4),
+                    scales=w1_plane[:, t * P : (t + 1) * P],
+                    in_=grouped[:, t * H : (t + 1) * H],
+                )
+            for h in range(2):
+                for t in range(PACK):
+                    nc.tensor.matmul_mx(
+                        out=banks[h][t][:],
+                        lhsT=w1_codes[:, t * P : (t + 1) * P].bitcast(FP8X4),
+                        lhsT_scale=w1_plane[:, t * P : (t + 1) * P],
+                        rhs=picked[h][:].bitcast(FP8X4),
+                        rhs_scale=x_plane[4 * z : P, h * HALF : (h + 1) * HALF],
+                        start=(z == 0),
+                        stop=(z == PASSES - 1),
+                    )
+
+        starts = [sum(CHUNKS[:c]) for c in range(len(CHUNKS))]
+        activated = {}
+
+        def add_and_gelu(c):
+            c0, width = starts[c], CHUNKS[c]
+            h, in_bank = divmod(c0, HALF)
+            piece, in_piece = divmod(c0, POS_W)
+            summed = ring.tile([P, PACK, width], F32, name="summed")
+            for t in range(PACK):
+                nc.vector.tensor_tensor(
+                    summed[:, t, :], banks[h][t][:, in_bank : in_bank + width], pos_sb[:, piece, t, in_piece : in_piece + width], ADD
+                )
+            hidden = ring.tile([P, PACK * width], BF16, name="hidden", align_bytes=64)
+            nc.scalar.activation(
+                hidden[:].rearrange("p (c i t) -> p c t i", i=4, t=PACK),
+                summed[:].rearrange("p t (c i) -> p c t i", i=4),
+                GELU,
+            )
+            activated[c] = hidden
+
+        def second_layer(c):
+            c0, width = starts[c], CHUNKS[c]
+            h_codes = ring.tile([P, width], U32, name="h_codes", align_bytes=64)
+            h_plane = ring.tile([P, width], U8, name="h_plane", align_bytes=64)
+            nc.vector.quantize_mx(out=h_codes[:].bitcast(FP8X4), scales=h_plane[:], in_=activated[c][:])
+            acc = psum.tile([P, width], F32, name="acc", tag=f"bank0{c % PACK}")
+            nc.tensor.matmul_mx(
+                out=acc[:],
+                lhsT=w2_codes[:].bitcast(FP4X4),
+                lhsT_scale=w2_plane[:],
+                rhs=h_codes[:].bitcast(FP8X4),
+                rhs_scale=h_plane[:],
+                start=True,
+                stop=True,
+            )
+            result = ring.tile([P, width], F32, name="result")
+            if c == len(CHUNKS) - 1:
+                nc.vector.tensor_copy(result[:], acc[:])
+            else:
+                nc.scalar.copy(result[:], acc[:])
+            nc.sync.dma_start(out[:, c0 : c0 + width], result[:])
+
+        for c in range(len(CHUNKS) + 2):
+            if c < len(CHUNKS):
+                add_and_gelu(c)
+            if c >= 2:
+                second_layer(c - 2)

@@ -21,19 +21,21 @@ PACK = 4
 PASSES = K // (P * PACK)
 HALF = 512
 POS_W = 256
-CHUNKS = (128, 128, 256, 256, 128, 128)
-SCALAR_M = (64, 48)
+GELU_WIDTHS = (128, 128, 256, 256, 128, 128)
+OUT_WIDTHS = (256, 256, 256, 128, 128)
 
 
 def tile_picked_phpq_gelu_p_kernel(tc, x_words, x_scales, w1, w2_words, w2_scales, pos, offs, out):
     nc = tc.nc
     with ExitStack() as ctx:
         keep = ctx.enter_context(tc.tile_pool(name="keep", bufs=1))
-        ring = ctx.enter_context(tc.tile_pool(name="ring", bufs=3))
+        ring = ctx.enter_context(tc.tile_pool(name="ring", bufs=6))
         psum = ctx.enter_context(tc.psum_pool(name="psum", bufs=1))
 
         lists = keep.tile([P, S // 16], U16, name="lists")
         nc.sync.dma_start(lists[:], offs)
+        w2_codes = keep.tile([P, 2 * N], U8, name="w2_codes", align_bytes=64)
+        nc.sync.dma_start(w2_codes[:].bitcast(I32), w2_words[0].bitcast(I32))
 
         scale_table = keep.tile([P, T], U8, name="scale_table", tag="early_a", align_bytes=64)
         nc.vector.memset(scale_table[:].bitcast(I32), 0)
@@ -46,10 +48,8 @@ def tile_picked_phpq_gelu_p_kernel(tc, x_words, x_scales, w1, w2_words, w2_scale
         nc.vector.memset(warm[:, 0:1], 0.0)
         nc.scalar.activation(warm[:, 1:2], warm[:, 0:1], GELU)
 
-        w2_codes = keep.tile([P, 2 * N], U8, name="w2_codes", align_bytes=64)
         w2_plane = keep.tile([P, N], U8, name="w2_plane", align_bytes=64)
         nc.gpsimd.memset(w2_plane[:].bitcast(I32), 0)
-        nc.gpsimd.dma_start(w2_codes[:].bitcast(I32), w2_words[0].bitcast(I32))
         for q in range(4):
             nc.gpsimd.dma_start(w2_plane[32 * q : 32 * q + 4, :].bitcast(I32), w2_scales[0, 4 * q : 4 * q + 4, :].bitcast(I32))
 
@@ -61,66 +61,74 @@ def tile_picked_phpq_gelu_p_kernel(tc, x_words, x_scales, w1, w2_words, w2_scale
             if z == 0:
                 raw = keep.tile([P, PACK, H], F32, name="w1_raw0")
                 nc.sync.dma_start(raw[:], w1[:512, :].rearrange("(p j) c -> p j c", j=PACK))
-                w1_raw.append(raw)
+                w1_raw.append(raw[:])
 
-        picked_scales = keep.tile([P, S], U8, name="picked_scales", tag="early_b", align_bytes=64)
+        picked_scales = keep.tile([P, S], U8, name="picked_scales", align_bytes=64)
         nc.vector.tensor_copy(picked_scales[:], scale_table[:].indirect(lists[:]))
+        late = keep.tile([P, PACK * (H + S)], F32, name="late", tag="early_a", align_bytes=64)
+        w1_raw.append(late[:, : PACK * H].rearrange("p (j c) -> p j c", j=PACK))
+        w1_rows = w1[512:, :].rearrange("(p j) c -> p j c", j=PACK)
+        nc.sync.dma_start(w1_raw[1][:, :1], w1_rows[:, :1])
         x_plane = keep.tile([P, S], U8, name="x_plane", align_bytes=64)
         nc.vector.tensor_copy(x_plane[:].bitcast(I32), picked_scales[:].bitcast(I32))
         for z in range(PASSES):
             for s in range(2):
-                nc.scalar.dma_start(
+                nc.sync.dma_start(
                     x_plane[4 * z + 2 + s : P : 32, :].bitcast(I32),
                     picked_scales[16 + 4 * z + s : P : 32, :].bitcast(I32),
                 )
 
-        raw = keep.tile([P, PACK, H], F32, name="w1_raw1", tag="early_a", align_bytes=64)
-        nc.sync.dma_start(raw[:], w1[512:, :].rearrange("(p j) c -> p j c", j=PACK))
-        w1_raw.append(raw)
-
-        pos_sb = keep.tile([P, S // POS_W, PACK, POS_W], F32, name="pos_sb", tag="early_b", align_bytes=64)
+        nc.sync.dma_start(w1_raw[1][:, 1:], w1_rows[:, 1:])
+        pos_sb = late[:, PACK * H :].rearrange("p (g t c) -> p g t c", t=PACK, c=POS_W)
         pos_rows = pos.rearrange("(p t) c -> p t c", t=PACK)
-        for c in range(S // POS_W):
-            nc.sync.dma_start(pos_sb[:, c], pos_rows[:, :, c * POS_W : (c + 1) * POS_W])
+        for g in range(S // POS_W):
+            nc.sync.dma_start(pos_sb[:, g], pos_rows[:, :, g * POS_W : (g + 1) * POS_W])
 
-        banks = [[psum.tile([P, HALF], F32, name=f"bank{h}{t}", tag=f"bank{h}{t}") for t in range(PACK)] for h in range(2)]
-        for z in range(PASSES):
-            picked = []
+        picked, w1_codes, w1_plane = {}, {}, {}
+
+        def gather_words(z):
             for h in range(2):
                 words = keep.tile([P, HALF], U32, name=f"picked{z}{h}", align_bytes=64)
                 nc.vector.tensor_copy(words[:], word_table[z][:].bitcast(U32).indirect(lists[:, 32 * h : 32 * (h + 1)]))
-                picked.append(words)
-            grouped = keep.tile([P, PACK * H], BF16, name=f"w1_grouped{z}", align_bytes=64)
-            dst = grouped[:].rearrange("p (t m j) -> p m j t", t=PACK, j=PACK)
-            src = w1_raw[z][:].rearrange("p j (m t) -> p m j t", t=PACK)
-            m_split = SCALAR_M[z]
-            nc.scalar.copy(dst[:, :m_split], src[:, :m_split])
-            nc.vector.tensor_copy(dst[:, m_split:], src[:, m_split:])
-            w1_codes = keep.tile([P, H], U32, name=f"w1_codes{z}", align_bytes=64)
-            w1_plane = keep.tile([P, H], U8, name=f"w1_plane{z}", align_bytes=64)
-            for t in range(PACK):
-                nc.vector.quantize_mx(
-                    out=w1_codes[:, t * P : (t + 1) * P].bitcast(FP8X4),
-                    scales=w1_plane[:, t * P : (t + 1) * P],
-                    in_=grouped[:, t * H : (t + 1) * H],
+                picked[z, h] = words
+
+        def quantize_w1(z):
+            for u, engine_copy in enumerate((nc.vector.tensor_copy, nc.scalar.copy)):
+                grouped = keep.tile([P, 2 * H], BF16, name=f"w1_grouped{z}{u}", align_bytes=64)
+                engine_copy(
+                    grouped[:].rearrange("p (e m j) -> p m j e", e=2, j=PACK),
+                    w1_raw[z].rearrange("p j (m u e) -> p u m j e", u=2, e=2)[:, u],
                 )
-            for h in range(2):
+                codes = keep.tile([P, 2 * P], U32, name=f"w1_codes{z}{u}", align_bytes=64)
+                plane = keep.tile([P, 2 * P], U8, name=f"w1_plane{z}{u}", align_bytes=64)
+                nc.vector.quantize_mx(out=codes[:].bitcast(FP8X4), scales=plane[:], in_=grouped[:])
+                for e in range(2):
+                    w1_codes[z, 2 * u + e] = codes[:, e * P : (e + 1) * P]
+                    w1_plane[z, 2 * u + e] = plane[:, e * P : (e + 1) * P]
+
+        gather_words(0)
+        quantize_w1(0)
+
+        gather_words(1)
+        quantize_w1(1)
+
+        banks = [[psum.tile([P, HALF], F32, name=f"bank{h}{t}", tag=f"bank{h}{t}") for t in range(PACK)] for h in range(2)]
+        for h in range(2):
+            for z in range(PASSES):
                 for t in range(PACK):
                     nc.tensor.matmul_mx(
                         out=banks[h][t][:],
-                        lhsT=w1_codes[:, t * P : (t + 1) * P].bitcast(FP8X4),
-                        lhsT_scale=w1_plane[:, t * P : (t + 1) * P],
-                        rhs=picked[h][:].bitcast(FP8X4),
+                        lhsT=w1_codes[z, t].bitcast(FP8X4),
+                        lhsT_scale=w1_plane[z, t],
+                        rhs=picked[z, h][:].bitcast(FP8X4),
                         rhs_scale=x_plane[4 * z : P, h * HALF : (h + 1) * HALF],
                         start=(z == 0),
                         stop=(z == PASSES - 1),
                     )
 
-        starts = [sum(CHUNKS[:c]) for c in range(len(CHUNKS))]
-        activated = {}
-
-        def add_and_gelu(c):
-            c0, width = starts[c], CHUNKS[c]
+        hidden = keep.tile([P, PACK * S], BF16, name="hidden", align_bytes=64)
+        c0 = 0
+        for width in GELU_WIDTHS:
             h, in_bank = divmod(c0, HALF)
             piece, in_piece = divmod(c0, POS_W)
             summed = ring.tile([P, PACK, width], F32, name="summed")
@@ -128,20 +136,20 @@ def tile_picked_phpq_gelu_p_kernel(tc, x_words, x_scales, w1, w2_words, w2_scale
                 nc.vector.tensor_tensor(
                     summed[:, t, :], banks[h][t][:, in_bank : in_bank + width], pos_sb[:, piece, t, in_piece : in_piece + width], ADD
                 )
-            hidden = ring.tile([P, PACK * width], BF16, name="hidden", align_bytes=64)
             nc.scalar.activation(
-                hidden[:].rearrange("p (c i t) -> p c t i", i=4, t=PACK),
+                hidden[:, PACK * c0 : PACK * (c0 + width)].rearrange("p (c i t) -> p c t i", i=4, t=PACK),
                 summed[:].rearrange("p t (c i) -> p c t i", i=4),
                 GELU,
             )
-            activated[c] = hidden
+            c0 = c0 + width
 
-        def second_layer(c):
-            c0, width = starts[c], CHUNKS[c]
+        products = []
+        c0 = 0
+        for n, width in enumerate(OUT_WIDTHS):
             h_codes = ring.tile([P, width], U32, name="h_codes", align_bytes=64)
             h_plane = ring.tile([P, width], U8, name="h_plane", align_bytes=64)
-            nc.vector.quantize_mx(out=h_codes[:].bitcast(FP8X4), scales=h_plane[:], in_=activated[c][:])
-            acc = psum.tile([P, width], F32, name="acc", tag=f"bank0{c % PACK}")
+            nc.vector.quantize_mx(out=h_codes[:].bitcast(FP8X4), scales=h_plane[:], in_=hidden[:, PACK * c0 : PACK * (c0 + width)])
+            acc = psum.tile([P, width], F32, name="acc", tag=f"bank{n // PACK}{n % PACK}")
             nc.tensor.matmul_mx(
                 out=acc[:],
                 lhsT=w2_codes[:].bitcast(FP4X4),
@@ -151,15 +159,16 @@ def tile_picked_phpq_gelu_p_kernel(tc, x_words, x_scales, w1, w2_words, w2_scale
                 start=True,
                 stop=True,
             )
-            result = ring.tile([P, width], F32, name="result")
-            if c == len(CHUNKS) - 1:
-                nc.vector.tensor_copy(result[:], acc[:])
-            else:
-                nc.scalar.copy(result[:], acc[:])
-            nc.sync.dma_start(out[:, c0 : c0 + width], result[:])
+            products.append((acc, c0, width))
+            c0 = c0 + width
 
-        for c in range(len(CHUNKS) + 2):
-            if c < len(CHUNKS):
-                add_and_gelu(c)
-            if c >= 2:
-                second_layer(c - 2)
+        result = keep.tile([P, S], F32, name="result")
+        stored = 0
+        for acc, c0, width in products:
+            if width == 128:
+                nc.vector.tensor_copy(result[:, c0 : c0 + width], acc[:])
+            else:
+                nc.scalar.copy(result[:, c0 : c0 + width], acc[:])
+            if c0 + width in (512, 768, 1024):
+                nc.sync.dma_start(out[:, stored : c0 + width], result[:, stored : c0 + width])
+                stored = c0 + width

@@ -18,79 +18,78 @@ ADD = mybir.AluOpType.add
 
 P = 128
 PACK = 4
-PASSES = K // (P * PACK)
+K_PASS = P * PACK
+PASSES = K // K_PASS
+GROUP = 16
+QUADRANT = 32
 HALF = 512
-POS_W = 256
-GELU_WIDTHS = (128, 128, 256, 256, 128, 128)
-OUT_WIDTHS = (256, 256, 256, 128, 128)
+POS_WIDTH = 256
+GELU_WIDTHS = (128, 128, 128, 128, 128, 128, 128, 64, 64)
+GELU_BUFS = 5
+WIDE, NARROW = 256, 128
+OUT_WIDTHS = (WIDE, WIDE, WIDE, NARROW, NARROW)
+STORE_ENDS = (2 * WIDE, 3 * WIDE, S)
 
 
-def tile_picked_phpq_gelu_p_kernel(tc, x_words, x_scales, w1, w2_words, w2_scales, pos, offs, out):
+def tile_picked_phpq_gelu_p_kernel(
+    tc, x_words, x_scales, w1, w2_words, w2_scales, pos, offs, out
+):
     nc = tc.nc
     with ExitStack() as ctx:
         keep = ctx.enter_context(tc.tile_pool(name="keep", bufs=1))
-        ring = ctx.enter_context(tc.tile_pool(name="ring", bufs=6))
+        ring = ctx.enter_context(tc.tile_pool(name="ring", bufs=GELU_BUFS))
         psum = ctx.enter_context(tc.psum_pool(name="psum", bufs=1))
 
-        lists = keep.tile([P, S // 16], U16, name="lists")
+        lists = keep.tile([P, S // GROUP], U16, name="lists")
         nc.sync.dma_start(lists[:], offs)
         w2_codes = keep.tile([P, 2 * N], U8, name="w2_codes", align_bytes=64)
         nc.sync.dma_start(w2_codes[:].bitcast(I32), w2_words[0].bitcast(I32))
 
-        scale_table = keep.tile([P, T], U8, name="scale_table", tag="early_a", align_bytes=64)
+        scale_table = keep.tile([P, T], U8, name="scale_table", tag="scales_then_late", align_bytes=64)
         nc.vector.memset(scale_table[:].bitcast(I32), 0)
         for z in range(PASSES):
             rows = x_scales[z].rearrange("(g s) c -> s g c", s=2)
             for s in range(2):
-                nc.sync.dma_start(scale_table[4 * z + s : P : 16, :].bitcast(I32), rows[s].bitcast(I32))
+                nc.sync.dma_start(scale_table[4 * z + s : P : GROUP, :].bitcast(I32), rows[s].bitcast(I32))
 
-        warm = keep.tile([P, 2], F32, name="warm")
-        nc.vector.memset(warm[:, 0:1], 0.0)
-        nc.scalar.activation(warm[:, 1:2], warm[:, 0:1], GELU)
-
-        w2_plane = keep.tile([P, N], U8, name="w2_plane", align_bytes=64)
-        nc.gpsimd.memset(w2_plane[:].bitcast(I32), 0)
-        for q in range(4):
-            nc.gpsimd.dma_start(w2_plane[32 * q : 32 * q + 4, :].bitcast(I32), w2_scales[0, 4 * q : 4 * q + 4, :].bitcast(I32))
-
-        word_table, w1_raw = [], []
-        for z in range(PASSES):
-            table = keep.tile([P, T], I32, name=f"word_table{z}", align_bytes=64)
-            nc.sync.dma_start(table[:], x_words[z].rearrange("p c r -> p (c r)").bitcast(I32))
-            word_table.append(table)
-            if z == 0:
-                raw = keep.tile([P, PACK, H], F32, name="w1_raw0")
-                nc.sync.dma_start(raw[:], w1[:512, :].rearrange("(p j) c -> p j c", j=PACK))
-                w1_raw.append(raw[:])
+        w1_rows = [w1[z * K_PASS : (z + 1) * K_PASS, :].rearrange("(p j) c -> p j c", j=PACK) for z in range(PASSES)]
+        word_table = [keep.tile([P, T], I32, name=f"word_table{z}", tag=f"table{z}", align_bytes=64) for z in range(PASSES)]
+        w1_first = keep.tile([P, PACK, H], F32, name="w1_first")
+        nc.sync.dma_start(word_table[0][:], x_words[0].rearrange("p c r -> p (c r)").bitcast(I32))
+        nc.sync.dma_start(w1_first[:], w1_rows[0])
+        nc.sync.dma_start(word_table[1][:], x_words[1].rearrange("p c r -> p (c r)").bitcast(I32))
 
         picked_scales = keep.tile([P, S], U8, name="picked_scales", align_bytes=64)
         nc.vector.tensor_copy(picked_scales[:], scale_table[:].indirect(lists[:]))
-        late = keep.tile([P, PACK * (H + S)], F32, name="late", tag="early_a", align_bytes=64)
-        w1_raw.append(late[:, : PACK * H].rearrange("p (j c) -> p j c", j=PACK))
-        w1_rows = w1[512:, :].rearrange("(p j) c -> p j c", j=PACK)
-        nc.sync.dma_start(w1_raw[1][:, :1], w1_rows[:, :1])
+
+        late = keep.tile([P, PACK * (H + S)], F32, name="late", tag="scales_then_late", align_bytes=64)
+        w1_raw = [w1_first[:], late[:, : PACK * H].rearrange("p (j c) -> p j c", j=PACK)]
+        nc.sync.dma_start(w1_raw[1][:, :1], w1_rows[1][:, :1])
+
         x_plane = keep.tile([P, S], U8, name="x_plane", align_bytes=64)
         nc.vector.tensor_copy(x_plane[:].bitcast(I32), picked_scales[:].bitcast(I32))
         for z in range(PASSES):
             for s in range(2):
                 nc.sync.dma_start(
-                    x_plane[4 * z + 2 + s : P : 32, :].bitcast(I32),
-                    picked_scales[16 + 4 * z + s : P : 32, :].bitcast(I32),
+                    x_plane[4 * z + 2 + s : P : QUADRANT, :].bitcast(I32),
+                    picked_scales[GROUP + 4 * z + s : P : QUADRANT, :].bitcast(I32),
                 )
 
-        nc.sync.dma_start(w1_raw[1][:, 1:], w1_rows[:, 1:])
-        pos_sb = late[:, PACK * H :].rearrange("p (g t c) -> p g t c", t=PACK, c=POS_W)
+        nc.sync.dma_start(w1_raw[1][:, 1:], w1_rows[1][:, 1:])
+        pos_sb = late[:, PACK * H :].rearrange("p (g t c) -> p g t c", t=PACK, c=POS_WIDTH)
         pos_rows = pos.rearrange("(p t) c -> p t c", t=PACK)
-        for g in range(S // POS_W):
-            nc.sync.dma_start(pos_sb[:, g], pos_rows[:, :, g * POS_W : (g + 1) * POS_W])
+        for g in range(S // POS_WIDTH):
+            nc.sync.dma_start(pos_sb[:, g], pos_rows[:, :, g * POS_WIDTH : (g + 1) * POS_WIDTH])
 
         picked, w1_codes, w1_plane = {}, {}, {}
 
         def gather_words(z):
-            for h in range(2):
-                words = keep.tile([P, HALF], U32, name=f"picked{z}{h}", align_bytes=64)
-                nc.vector.tensor_copy(words[:], word_table[z][:].bitcast(U32).indirect(lists[:, 32 * h : 32 * (h + 1)]))
-                picked[z, h] = words
+            columns = HALF // GROUP
+            for half in range(S // HALF):
+                words = keep.tile([P, HALF], U32, name=f"picked{z}{half}", align_bytes=64)
+                offsets = lists[:, columns * half : columns * (half + 1)]
+                nc.vector.tensor_copy(words[:], word_table[z][:].bitcast(U32).indirect(offsets))
+                picked[z, half] = words
 
         def quantize_w1(z):
             for u, engine_copy in enumerate((nc.vector.tensor_copy, nc.scalar.copy)):
@@ -107,49 +106,62 @@ def tile_picked_phpq_gelu_p_kernel(tc, x_words, x_scales, w1, w2_words, w2_scale
                     w1_plane[z, 2 * u + e] = plane[:, e * P : (e + 1) * P]
 
         gather_words(0)
-        quantize_w1(0)
 
+        w2_plane = keep.tile([P, N], U8, name="w2_plane", tag="table0", align_bytes=64)
+        nc.gpsimd.memset(w2_plane[:].bitcast(I32), 0)
+        for q in range(P // QUADRANT):
+            nc.sync.dma_start(
+                w2_plane[QUADRANT * q : QUADRANT * q + 4, :].bitcast(I32), w2_scales[0, 4 * q : 4 * q + 4, :].bitcast(I32)
+            )
+
+        quantize_w1(0)
         gather_words(1)
         quantize_w1(1)
 
-        banks = [[psum.tile([P, HALF], F32, name=f"bank{h}{t}", tag=f"bank{h}{t}") for t in range(PACK)] for h in range(2)]
-        for h in range(2):
-            for z in range(PASSES):
-                for t in range(PACK):
-                    nc.tensor.matmul_mx(
-                        out=banks[h][t][:],
-                        lhsT=w1_codes[z, t].bitcast(FP8X4),
-                        lhsT_scale=w1_plane[z, t],
-                        rhs=picked[z, h][:].bitcast(FP8X4),
-                        rhs_scale=x_plane[4 * z : P, h * HALF : (h + 1) * HALF],
-                        start=(z == 0),
-                        stop=(z == PASSES - 1),
-                    )
+        banks = [[psum.tile([P, HALF], F32, name=f"bank{half}{t}", tag=f"bank{half}{t}") for t in range(PACK)] for half in range(2)]
+        orders = (
+            [(z, t) for z in (0, 1) for t in range(PACK)],
+            [(z, t) for t in range(PACK) for z in (1, 0)],
+        )
+        for half, order in enumerate(orders):
+            opening_pass = order[0][0]
+            for z, t in order:
+                nc.tensor.matmul_mx(
+                    out=banks[half][t][:],
+                    lhsT=w1_codes[z, t].bitcast(FP8X4),
+                    lhsT_scale=w1_plane[z, t],
+                    rhs=picked[z, half][:].bitcast(FP8X4),
+                    rhs_scale=x_plane[4 * z : P, half * HALF : (half + 1) * HALF],
+                    start=(z == opening_pass),
+                    stop=(z != opening_pass),
+                )
 
         hidden = keep.tile([P, PACK * S], BF16, name="hidden", align_bytes=64)
-        c0 = 0
+        first = 0
         for width in GELU_WIDTHS:
-            h, in_bank = divmod(c0, HALF)
-            piece, in_piece = divmod(c0, POS_W)
+            half, in_bank = divmod(first, HALF)
+            g, in_load = divmod(first, POS_WIDTH)
             summed = ring.tile([P, PACK, width], F32, name="summed")
             for t in range(PACK):
                 nc.vector.tensor_tensor(
-                    summed[:, t, :], banks[h][t][:, in_bank : in_bank + width], pos_sb[:, piece, t, in_piece : in_piece + width], ADD
+                    summed[:, t, :], banks[half][t][:, in_bank : in_bank + width], pos_sb[:, g, t, in_load : in_load + width], ADD
                 )
             nc.scalar.activation(
-                hidden[:, PACK * c0 : PACK * (c0 + width)].rearrange("p (c i t) -> p c t i", i=4, t=PACK),
-                summed[:].rearrange("p t (c i) -> p c t i", i=4),
+                hidden[:, PACK * first : PACK * (first + width)].rearrange("p (c n t) -> p c t n", n=4, t=PACK),
+                summed[:].rearrange("p t (c n) -> p c t n", n=4),
                 GELU,
             )
-            c0 = c0 + width
+            first = first + width
 
         products = []
-        c0 = 0
-        for n, width in enumerate(OUT_WIDTHS):
+        first = 0
+        for piece, width in enumerate(OUT_WIDTHS):
             h_codes = ring.tile([P, width], U32, name="h_codes", align_bytes=64)
             h_plane = ring.tile([P, width], U8, name="h_plane", align_bytes=64)
-            nc.vector.quantize_mx(out=h_codes[:].bitcast(FP8X4), scales=h_plane[:], in_=hidden[:, PACK * c0 : PACK * (c0 + width)])
-            acc = psum.tile([P, width], F32, name="acc", tag=f"bank{n // PACK}{n % PACK}")
+            nc.vector.quantize_mx(
+                out=h_codes[:].bitcast(FP8X4), scales=h_plane[:], in_=hidden[:, PACK * first : PACK * (first + width)]
+            )
+            acc = psum.tile([P, width], F32, name="acc", tag=f"bank{piece // PACK}{piece % PACK}")
             nc.tensor.matmul_mx(
                 out=acc[:],
                 lhsT=w2_codes[:].bitcast(FP4X4),
@@ -159,16 +171,15 @@ def tile_picked_phpq_gelu_p_kernel(tc, x_words, x_scales, w1, w2_words, w2_scale
                 start=True,
                 stop=True,
             )
-            products.append((acc, c0, width))
-            c0 = c0 + width
+            products.append((acc, first, width))
+            first = first + width
 
         result = keep.tile([P, S], F32, name="result")
         stored = 0
-        for acc, c0, width in products:
-            if width == 128:
-                nc.vector.tensor_copy(result[:, c0 : c0 + width], acc[:])
-            else:
-                nc.scalar.copy(result[:, c0 : c0 + width], acc[:])
-            if c0 + width in (512, 768, 1024):
-                nc.sync.dma_start(out[:, stored : c0 + width], result[:, stored : c0 + width])
-                stored = c0 + width
+        for acc, first, width in products:
+            end = first + width
+            engine_copy = nc.scalar.copy if width == WIDE else nc.vector.tensor_copy
+            engine_copy(result[:, first:end], acc[:])
+            if end in STORE_ENDS:
+                nc.sync.dma_start(out[:, stored:end], result[:, stored:end])
+                stored = end

@@ -23,7 +23,8 @@ PASSES = K // K_PASS
 GROUP = 16
 QUADRANT = 32
 HALF = 512
-POS_WIDTH = 256
+TABLE_HEAD = 256
+POS_WIDTHS = (256, 512, 128, 128)
 GELU_WIDTHS = (128, 128, 128, 128, 128, 128, 128, 64, 64)
 GELU_BUFS = 5
 WIDE, NARROW = 256, 128
@@ -37,34 +38,42 @@ def tile_picked_phpq_gelu_p_kernel(
     nc = tc.nc
     with ExitStack() as ctx:
         keep = ctx.enter_context(tc.tile_pool(name="keep", bufs=1))
+        after = ctx.enter_context(tc.tile_pool(name="after", bufs=1))
         ring = ctx.enter_context(tc.tile_pool(name="ring", bufs=GELU_BUFS))
         psum = ctx.enter_context(tc.psum_pool(name="psum", bufs=1))
 
         lists = keep.tile([P, S // GROUP], U16, name="lists")
         nc.sync.dma_start(lists[:], offs)
-        w2_codes = keep.tile([P, 2 * N], U8, name="w2_codes", align_bytes=64)
-        nc.sync.dma_start(w2_codes[:].bitcast(I32), w2_words[0].bitcast(I32))
+        word_table = [keep.tile([P, T], I32, name=f"word_table{z}", tag=f"table{z}", align_bytes=64) for z in range(PASSES)]
+        table_rows = [x_words[z].rearrange("p c r -> p (c r)").bitcast(I32) for z in range(PASSES)]
+        for first in range(0, 2 * TABLE_HEAD, TABLE_HEAD):
+            nc.sync.dma_start(word_table[0][:, first : first + TABLE_HEAD], table_rows[0][:, first : first + TABLE_HEAD])
 
-        scale_table = keep.tile([P, T], U8, name="scale_table", tag="scales_then_late", align_bytes=64)
-        nc.vector.memset(scale_table[:].bitcast(I32), 0)
-        for z in range(PASSES):
+        scale_table = after.tile([P, T], U8, name="scale_table", align_bytes=64, offset=0)
+        nc.vector.memset(scale_table[:, : T // 2].bitcast(I32), 0)
+        nc.gpsimd.memset(scale_table[:, T // 2 :].bitcast(I32), 0)
+        for z, queue in enumerate((nc.sync, nc.scalar)):
             rows = x_scales[z].rearrange("(g s) c -> s g c", s=2)
             for s in range(2):
-                nc.sync.dma_start(scale_table[4 * z + s : P : GROUP, :].bitcast(I32), rows[s].bitcast(I32))
+                queue.dma_start(scale_table[4 * z + s : P : GROUP, :].bitcast(I32), rows[s].bitcast(I32))
+
+        warm = keep.tile([P, 16], F32, name="warm")
+        nc.vector.memset(warm[:, :8], 0.0)
+        nc.scalar.activation(warm[:, 8:], warm[:, :8], GELU)
 
         w1_rows = [w1[z * K_PASS : (z + 1) * K_PASS, :].rearrange("(p j) c -> p j c", j=PACK) for z in range(PASSES)]
-        word_table = [keep.tile([P, T], I32, name=f"word_table{z}", tag=f"table{z}", align_bytes=64) for z in range(PASSES)]
         w1_first = keep.tile([P, PACK, H], F32, name="w1_first")
-        nc.sync.dma_start(word_table[0][:], x_words[0].rearrange("p c r -> p (c r)").bitcast(I32))
+        nc.sync.dma_start(word_table[0][:, 2 * TABLE_HEAD :], table_rows[0][:, 2 * TABLE_HEAD :])
         nc.sync.dma_start(w1_first[:], w1_rows[0])
-        nc.sync.dma_start(word_table[1][:], x_words[1].rearrange("p c r -> p (c r)").bitcast(I32))
+        nc.sync.dma_start(word_table[1][:], table_rows[1])
 
         picked_scales = keep.tile([P, S], U8, name="picked_scales", align_bytes=64)
         nc.vector.tensor_copy(picked_scales[:], scale_table[:].indirect(lists[:]))
 
-        late = keep.tile([P, PACK * (H + S)], F32, name="late", tag="scales_then_late", align_bytes=64)
+        late = after.tile([P, PACK * (H + S)], F32, name="late", align_bytes=64, offset=2 * N)
         w1_raw = [w1_first[:], late[:, : PACK * H].rearrange("p (j c) -> p j c", j=PACK)]
-        nc.sync.dma_start(w1_raw[1][:, :1], w1_rows[1][:, :1])
+        w2_codes = after.tile([P, 2 * N], U8, name="w2_codes", align_bytes=64, offset=0)
+        nc.sync.dma_start(w2_codes[:].bitcast(I32), w2_words[0].bitcast(I32))
 
         x_plane = keep.tile([P, S], U8, name="x_plane", align_bytes=64)
         nc.vector.tensor_copy(x_plane[:].bitcast(I32), picked_scales[:].bitcast(I32))
@@ -75,11 +84,16 @@ def tile_picked_phpq_gelu_p_kernel(
                     picked_scales[GROUP + 4 * z + s : P : QUADRANT, :].bitcast(I32),
                 )
 
-        nc.sync.dma_start(w1_raw[1][:, 1:], w1_rows[1][:, 1:])
-        pos_sb = late[:, PACK * H :].rearrange("p (g t c) -> p g t c", t=PACK, c=POS_WIDTH)
+        nc.sync.dma_start(w1_raw[1], w1_rows[1])
         pos_rows = pos.rearrange("(p t) c -> p t c", t=PACK)
-        for g in range(S // POS_WIDTH):
-            nc.sync.dma_start(pos_sb[:, g], pos_rows[:, :, g * POS_WIDTH : (g + 1) * POS_WIDTH])
+        pos_of = {}
+        first = 0
+        for width in POS_WIDTHS:
+            part = late[:, PACK * (H + first) : PACK * (H + first + width)].rearrange("p (t c) -> p t c", t=PACK)
+            nc.sync.dma_start(part, pos_rows[:, :, first : first + width])
+            for column in range(0, width, 64):
+                pos_of[first + column] = part[:, :, column:]
+            first = first + width
 
         picked, w1_codes, w1_plane = {}, {}, {}
 
@@ -91,8 +105,8 @@ def tile_picked_phpq_gelu_p_kernel(
                 nc.vector.tensor_copy(words[:], word_table[z][:].bitcast(U32).indirect(offsets))
                 picked[z, half] = words
 
-        def quantize_w1(z):
-            for u, engine_copy in enumerate((nc.vector.tensor_copy, nc.scalar.copy)):
+        def quantize_w1(z, copies):
+            for u, engine_copy in enumerate(copies):
                 grouped = keep.tile([P, 2 * H], BF16, name=f"w1_grouped{z}{u}", align_bytes=64)
                 engine_copy(
                     grouped[:].rearrange("p (e m j) -> p m j e", e=2, j=PACK),
@@ -114,9 +128,9 @@ def tile_picked_phpq_gelu_p_kernel(
                 w2_plane[QUADRANT * q : QUADRANT * q + 4, :].bitcast(I32), w2_scales[0, 4 * q : 4 * q + 4, :].bitcast(I32)
             )
 
-        quantize_w1(0)
+        quantize_w1(0, (nc.scalar.copy, nc.scalar.copy))
         gather_words(1)
-        quantize_w1(1)
+        quantize_w1(1, (nc.vector.tensor_copy, nc.scalar.copy))
 
         banks = [[psum.tile([P, HALF], F32, name=f"bank{half}{t}", tag=f"bank{half}{t}") for t in range(PACK)] for half in range(2)]
         orders = (
@@ -140,11 +154,10 @@ def tile_picked_phpq_gelu_p_kernel(
         first = 0
         for width in GELU_WIDTHS:
             half, in_bank = divmod(first, HALF)
-            g, in_load = divmod(first, POS_WIDTH)
             summed = ring.tile([P, PACK, width], F32, name="summed")
             for t in range(PACK):
                 nc.vector.tensor_tensor(
-                    summed[:, t, :], banks[half][t][:, in_bank : in_bank + width], pos_sb[:, g, t, in_load : in_load + width], ADD
+                    summed[:, t, :], banks[half][t][:, in_bank : in_bank + width], pos_of[first][:, t, :width], ADD
                 )
             nc.scalar.activation(
                 hidden[:, PACK * first : PACK * (first + width)].rearrange("p (c n t) -> p c t n", n=4, t=PACK),

@@ -23,13 +23,15 @@ PASSES = K // K_PASS
 GROUP = 16
 QUADRANT = 32
 HALF = 512
+STRETCHES = ((0, 256, 0), (256, 512, 1), (768, 256, 0))
+SCALAR_COLUMNS = 56
 TABLE_HEAD = 256
 POS_WIDTHS = (256, 512, 128, 128)
 GELU_WIDTHS = (128, 128, 128, 128, 128, 128, 128, 64, 64)
 GELU_BUFS = 5
 WIDE, NARROW = 256, 128
 OUT_WIDTHS = (WIDE, WIDE, WIDE, NARROW, NARROW)
-STORE_ENDS = (2 * WIDE, 3 * WIDE, S)
+STORE_ENDS = (WIDE, 2 * WIDE, 3 * WIDE, 3 * WIDE + NARROW, S)
 
 
 def tile_picked_phpq_gelu_p_kernel(
@@ -98,26 +100,31 @@ def tile_picked_phpq_gelu_p_kernel(
         picked, w1_codes, w1_plane = {}, {}, {}
 
         def gather_words(z):
-            columns = HALF // GROUP
-            for half in range(S // HALF):
-                words = keep.tile([P, HALF], U32, name=f"picked{z}{half}", align_bytes=64)
-                offsets = lists[:, columns * half : columns * (half + 1)]
-                nc.vector.tensor_copy(words[:], word_table[z][:].bitcast(U32).indirect(offsets))
-                picked[z, half] = words
+            words = keep.tile([P, S], U32, name=f"picked{z}", align_bytes=64)
+            for first in range(0, S, HALF):
+                offsets = lists[:, first // GROUP : (first + HALF) // GROUP]
+                nc.vector.tensor_copy(words[:, first : first + HALF], word_table[z][:].bitcast(U32).indirect(offsets))
+            picked[z] = words
 
-        def quantize_w1(z, copies):
-            for u, engine_copy in enumerate(copies):
-                grouped = keep.tile([P, 2 * H], BF16, name=f"w1_grouped{z}{u}", align_bytes=64)
-                engine_copy(
-                    grouped[:].rearrange("p (e m j) -> p m j e", e=2, j=PACK),
-                    w1_raw[z].rearrange("p j (m u e) -> p u m j e", u=2, e=2)[:, u],
-                )
-                codes = keep.tile([P, 2 * P], U32, name=f"w1_codes{z}{u}", align_bytes=64)
-                plane = keep.tile([P, 2 * P], U8, name=f"w1_plane{z}{u}", align_bytes=64)
-                nc.vector.quantize_mx(out=codes[:].bitcast(FP8X4), scales=plane[:], in_=grouped[:])
-                for e in range(2):
-                    w1_codes[z, 2 * u + e] = codes[:, e * P : (e + 1) * P]
-                    w1_plane[z, 2 * u + e] = plane[:, e * P : (e + 1) * P]
+        grouped = {
+            (z, u): keep.tile([P, 2 * H], BF16, name=f"w1_grouped{z}{u}", align_bytes=64)
+            for z in range(PASSES)
+            for u in range(2)
+        }
+
+        def cast_w1(engine_copy, z, u, columns):
+            engine_copy(
+                grouped[z, u][:].rearrange("p (e m j) -> p m j e", e=2, j=PACK)[:, columns],
+                w1_raw[z].rearrange("p j (m u e) -> p u m j e", u=2, e=2)[:, u, columns],
+            )
+
+        def quantize_w1(z, u, tag):
+            codes = keep.tile([P, 2 * P], U32, name=f"w1_codes{z}{u}", tag=tag, align_bytes=64)
+            plane = keep.tile([P, 2 * P], U8, name=f"w1_plane{z}{u}", align_bytes=64)
+            nc.vector.quantize_mx(out=codes[:].bitcast(FP8X4), scales=plane[:], in_=grouped[z, u][:])
+            for e in range(2):
+                w1_codes[z, 2 * u + e] = codes[:, e * P : (e + 1) * P]
+                w1_plane[z, 2 * u + e] = plane[:, e * P : (e + 1) * P]
 
         gather_words(0)
 
@@ -128,36 +135,52 @@ def tile_picked_phpq_gelu_p_kernel(
                 w2_plane[QUADRANT * q : QUADRANT * q + 4, :].bitcast(I32), w2_scales[0, 4 * q : 4 * q + 4, :].bitcast(I32)
             )
 
-        quantize_w1(0, (nc.scalar.copy, nc.scalar.copy))
+        for u in range(2):
+            cast_w1(nc.scalar.copy, 0, u, slice(0, P))
+        quantize_w1(0, 0, "codes00")
         gather_words(1)
-        quantize_w1(1, (nc.vector.tensor_copy, nc.scalar.copy))
+        quantize_w1(0, 1, "table1")
+        for u in range(2):
+            cast_w1(nc.scalar.copy, 1, u, slice(0, SCALAR_COLUMNS))
+            cast_w1(nc.vector.tensor_copy, 1, u, slice(SCALAR_COLUMNS, P))
+        for u in range(2):
+            quantize_w1(1, u, f"codes1{u}")
 
-        banks = [[psum.tile([P, HALF], F32, name=f"bank{half}{t}", tag=f"bank{half}{t}") for t in range(PACK)] for half in range(2)]
-        orders = (
-            [(z, t) for z in (0, 1) for t in range(PACK)],
-            [(z, t) for t in range(PACK) for z in (1, 0)],
-        )
-        for half, order in enumerate(orders):
-            opening_pass = order[0][0]
-            for z, t in order:
+        banks = {}
+
+        def products(z, stretch, ts=range(PACK)):
+            first, width, tags = stretch
+            for t in ts:
+                if z == 0:
+                    banks[first, t] = psum.tile([P, width], F32, name=f"bank{first}{t}", tag=f"bank{tags}{t}")
                 nc.tensor.matmul_mx(
-                    out=banks[half][t][:],
+                    out=banks[first, t][:],
                     lhsT=w1_codes[z, t].bitcast(FP8X4),
                     lhsT_scale=w1_plane[z, t],
-                    rhs=picked[z, half][:].bitcast(FP8X4),
-                    rhs_scale=x_plane[4 * z : P, half * HALF : (half + 1) * HALF],
-                    start=(z == opening_pass),
-                    stop=(z != opening_pass),
+                    rhs=picked[z][:, first : first + width].bitcast(FP8X4),
+                    rhs_scale=x_plane[4 * z : P, first : first + width],
+                    start=(z == 0),
+                    stop=(z == PASSES - 1),
                 )
+
+        for ts in ((0, 1), (2, 3)):
+            products(0, STRETCHES[0], ts)
+            products(0, STRETCHES[1], ts)
+        products(1, STRETCHES[0])
+        products(1, STRETCHES[1])
 
         hidden = keep.tile([P, PACK * S], BF16, name="hidden", align_bytes=64)
         first = 0
         for width in GELU_WIDTHS:
-            half, in_bank = divmod(first, HALF)
+            if first == STRETCHES[0][1]:
+                for z in range(PASSES):
+                    products(z, STRETCHES[2])
+            bank_first = max(stretch[0] for stretch in STRETCHES if stretch[0] <= first)
+            in_bank = first - bank_first
             summed = ring.tile([P, PACK, width], F32, name="summed")
             for t in range(PACK):
                 nc.vector.tensor_tensor(
-                    summed[:, t, :], banks[half][t][:, in_bank : in_bank + width], pos_of[first][:, t, :width], ADD
+                    summed[:, t, :], banks[bank_first, t][:, in_bank : in_bank + width], pos_of[first][:, t, :width], ADD
                 )
             nc.scalar.activation(
                 hidden[:, PACK * first : PACK * (first + width)].rearrange("p (c n t) -> p c t n", n=4, t=PACK),
@@ -174,7 +197,7 @@ def tile_picked_phpq_gelu_p_kernel(
             nc.vector.quantize_mx(
                 out=h_codes[:].bitcast(FP8X4), scales=h_plane[:], in_=hidden[:, PACK * first : PACK * (first + width)]
             )
-            acc = psum.tile([P, width], F32, name="acc", tag=f"bank{piece // PACK}{piece % PACK}")
+            acc = psum.tile([P, width], F32, name="acc", tag=f"bank{1 - piece // PACK}{piece % PACK}")
             nc.tensor.matmul_mx(
                 out=acc[:],
                 lhsT=w2_codes[:].bitcast(FP4X4),
@@ -191,7 +214,7 @@ def tile_picked_phpq_gelu_p_kernel(
         stored = 0
         for acc, first, width in products:
             end = first + width
-            engine_copy = nc.scalar.copy if width == WIDE else nc.vector.tensor_copy
+            engine_copy = nc.scalar.copy if end <= 2 * WIDE else nc.vector.tensor_copy
             engine_copy(result[:, first:end], acc[:])
             if end in STORE_ENDS:
                 nc.sync.dma_start(out[:, stored:end], result[:, stored:end])

@@ -25,8 +25,8 @@ QUADRANT = 32
 HALF = 512
 STRETCHES = ((0, 256, 0), (256, 512, 1), (768, 256, 0))
 SCALAR_COLUMNS = 56
-TABLE_HEAD = 256
-POS_WIDTHS = (256, 512, 128, 128)
+TABLE_HEAD = 512
+POS_WIDTHS = (256, 512, 256)
 GELU_WIDTHS = (128, 128, 128, 128, 128, 128, 128, 64, 64)
 GELU_BUFS = 5
 WIDE, NARROW = 256, 128
@@ -48,16 +48,14 @@ def tile_picked_phpq_gelu_p_kernel(
         nc.sync.dma_start(lists[:], offs)
         word_table = [keep.tile([P, T], I32, name=f"word_table{z}", tag=f"table{z}", align_bytes=64) for z in range(PASSES)]
         table_rows = [x_words[z].rearrange("p c r -> p (c r)").bitcast(I32) for z in range(PASSES)]
-        for first in range(0, 2 * TABLE_HEAD, TABLE_HEAD):
-            nc.sync.dma_start(word_table[0][:, first : first + TABLE_HEAD], table_rows[0][:, first : first + TABLE_HEAD])
+        nc.sync.dma_start(word_table[0][:, :TABLE_HEAD], table_rows[0][:, :TABLE_HEAD])
 
         scale_table = after.tile([P, T], U8, name="scale_table", align_bytes=64, offset=0)
-        nc.vector.memset(scale_table[:, : T // 2].bitcast(I32), 0)
-        nc.gpsimd.memset(scale_table[:, T // 2 :].bitcast(I32), 0)
-        for z, queue in enumerate((nc.sync, nc.scalar)):
+        nc.vector.memset(scale_table[:].bitcast(I32), 0)
+        for z in range(PASSES):
             rows = x_scales[z].rearrange("(g s) c -> s g c", s=2)
             for s in range(2):
-                queue.dma_start(scale_table[4 * z + s : P : GROUP, :].bitcast(I32), rows[s].bitcast(I32))
+                nc.sync.dma_start(scale_table[4 * z + s : P : GROUP, :].bitcast(I32), rows[s].bitcast(I32))
 
         warm = keep.tile([P, 16], F32, name="warm")
         nc.vector.memset(warm[:, :8], 0.0)
@@ -65,7 +63,7 @@ def tile_picked_phpq_gelu_p_kernel(
 
         w1_rows = [w1[z * K_PASS : (z + 1) * K_PASS, :].rearrange("(p j) c -> p j c", j=PACK) for z in range(PASSES)]
         w1_first = keep.tile([P, PACK, H], F32, name="w1_first")
-        nc.sync.dma_start(word_table[0][:, 2 * TABLE_HEAD :], table_rows[0][:, 2 * TABLE_HEAD :])
+        nc.sync.dma_start(word_table[0][:, TABLE_HEAD:], table_rows[0][:, TABLE_HEAD:])
         nc.sync.dma_start(w1_first[:], w1_rows[0])
         nc.sync.dma_start(word_table[1][:], table_rows[1])
 
@@ -135,11 +133,12 @@ def tile_picked_phpq_gelu_p_kernel(
                 w2_plane[QUADRANT * q : QUADRANT * q + 4, :].bitcast(I32), w2_scales[0, 4 * q : 4 * q + 4, :].bitcast(I32)
             )
 
+        cast_w1(nc.scalar.copy, 0, 0, slice(0, P))
+        cast_w1(nc.scalar.copy, 0, 1, slice(0, P // 2))
+        cast_w1(nc.vector.tensor_copy, 0, 1, slice(P // 2, P))
         for u in range(2):
-            cast_w1(nc.scalar.copy, 0, u, slice(0, P))
-        quantize_w1(0, 0, "codes00")
+            quantize_w1(0, u, f"codes0{u}")
         gather_words(1)
-        quantize_w1(0, 1, "table1")
         for u in range(2):
             cast_w1(nc.scalar.copy, 1, u, slice(0, SCALAR_COLUMNS))
             cast_w1(nc.vector.tensor_copy, 1, u, slice(SCALAR_COLUMNS, P))
@@ -148,9 +147,9 @@ def tile_picked_phpq_gelu_p_kernel(
 
         banks = {}
 
-        def products(z, stretch, ts=range(PACK)):
+        def products(z, stretch):
             first, width, tags = stretch
-            for t in ts:
+            for t in range(PACK):
                 if z == 0:
                     banks[first, t] = psum.tile([P, width], F32, name=f"bank{first}{t}", tag=f"bank{tags}{t}")
                 nc.tensor.matmul_mx(
@@ -163,11 +162,9 @@ def tile_picked_phpq_gelu_p_kernel(
                     stop=(z == PASSES - 1),
                 )
 
-        for ts in ((0, 1), (2, 3)):
-            products(0, STRETCHES[0], ts)
-            products(0, STRETCHES[1], ts)
-        products(1, STRETCHES[0])
-        products(1, STRETCHES[1])
+        for z in range(PASSES):
+            products(z, STRETCHES[0])
+            products(z, STRETCHES[1])
 
         hidden = keep.tile([P, PACK * S], BF16, name="hidden", align_bytes=64)
         first = 0

@@ -24,9 +24,10 @@ GROUP = 16
 QUADRANT = 32
 HALF = 512
 STRETCHES = ((0, 256, 0), (256, 512, 1), (768, 256, 0))
-SCALAR_COLUMNS = 56
+OUT_BANKS = ("bank02", "bank03", "bank10", "bank11", "bank12")
+SCALAR_COLUMNS = 64
 TABLE_HEAD = 512
-POS_WIDTHS = (256, 512, 256)
+POS_WIDTHS = (256, 256, 256, 256)
 GELU_WIDTHS = (128, 128, 128, 128, 128, 128, 128, 64, 64)
 GELU_BUFS = 5
 WIDE, NARROW = 256, 128
@@ -97,15 +98,16 @@ def tile_picked_phpq_gelu_p_kernel(
 
         picked, w1_codes, w1_plane = {}, {}, {}
 
-        def gather_words(z):
-            words = keep.tile([P, S], U32, name=f"picked{z}", align_bytes=64)
-            for first in range(0, S, HALF):
-                offsets = lists[:, first // GROUP : (first + HALF) // GROUP]
-                nc.vector.tensor_copy(words[:, first : first + HALF], word_table[z][:].bitcast(U32).indirect(offsets))
-            picked[z] = words
+        def gather_words(z, first, width, tag):
+            words = keep.tile([P, width], U32, name=f"picked{z}{first}", tag=tag, align_bytes=64)
+            offsets = lists[:, first // GROUP : (first + width) // GROUP]
+            nc.vector.tensor_copy(words[:], word_table[z][:].bitcast(U32).indirect(offsets))
+            for start, columns, tags in STRETCHES:
+                if first <= start < first + width:
+                    picked[z, start] = words[:, start - first : start - first + columns]
 
         grouped = {
-            (z, u): keep.tile([P, 2 * H], BF16, name=f"w1_grouped{z}{u}", align_bytes=64)
+            (z, u): keep.tile([P, 2 * H], BF16, name=f"w1_grouped{z}{u}", tag=f"grouped{z}{u}", align_bytes=64)
             for z in range(PASSES)
             for u in range(2)
         }
@@ -124,7 +126,7 @@ def tile_picked_phpq_gelu_p_kernel(
                 w1_codes[z, 2 * u + e] = codes[:, e * P : (e + 1) * P]
                 w1_plane[z, 2 * u + e] = plane[:, e * P : (e + 1) * P]
 
-        gather_words(0)
+        gather_words(0, 0, S, "picked0")
 
         w2_plane = keep.tile([P, N], U8, name="w2_plane", tag="table0", align_bytes=64)
         nc.gpsimd.memset(w2_plane[:].bitcast(I32), 0)
@@ -134,11 +136,11 @@ def tile_picked_phpq_gelu_p_kernel(
             )
 
         cast_w1(nc.scalar.copy, 0, 0, slice(0, P))
-        cast_w1(nc.scalar.copy, 0, 1, slice(0, P // 2))
-        cast_w1(nc.vector.tensor_copy, 0, 1, slice(P // 2, P))
+        cast_w1(nc.scalar.copy, 0, 1, slice(0, 3 * P // 4))
+        cast_w1(nc.vector.tensor_copy, 0, 1, slice(3 * P // 4, P))
         for u in range(2):
             quantize_w1(0, u, f"codes0{u}")
-        gather_words(1)
+        gather_words(1, 0, S, "picked1")
         for u in range(2):
             cast_w1(nc.scalar.copy, 1, u, slice(0, SCALAR_COLUMNS))
             cast_w1(nc.vector.tensor_copy, 1, u, slice(SCALAR_COLUMNS, P))
@@ -147,20 +149,23 @@ def tile_picked_phpq_gelu_p_kernel(
 
         banks = {}
 
+        def multiply(acc, z, t, first, width):
+            nc.tensor.matmul_mx(
+                out=acc,
+                lhsT=w1_codes[z, t].bitcast(FP8X4),
+                lhsT_scale=w1_plane[z, t],
+                rhs=picked[z, first].bitcast(FP8X4),
+                rhs_scale=x_plane[4 * z : P, first : first + width],
+                start=(z == 0),
+                stop=(z == PASSES - 1),
+            )
+
         def products(z, stretch):
             first, width, tags = stretch
             for t in range(PACK):
                 if z == 0:
                     banks[first, t] = psum.tile([P, width], F32, name=f"bank{first}{t}", tag=f"bank{tags}{t}")
-                nc.tensor.matmul_mx(
-                    out=banks[first, t][:],
-                    lhsT=w1_codes[z, t].bitcast(FP8X4),
-                    lhsT_scale=w1_plane[z, t],
-                    rhs=picked[z][:, first : first + width].bitcast(FP8X4),
-                    rhs_scale=x_plane[4 * z : P, first : first + width],
-                    start=(z == 0),
-                    stop=(z == PASSES - 1),
-                )
+                multiply(banks[first, t][:], z, t, first, width)
 
         for z in range(PASSES):
             products(z, STRETCHES[0])
@@ -170,15 +175,27 @@ def tile_picked_phpq_gelu_p_kernel(
         first = 0
         for width in GELU_WIDTHS:
             if first == STRETCHES[0][1]:
-                for z in range(PASSES):
-                    products(z, STRETCHES[2])
+                last_first, last_width, tags = STRETCHES[2]
+                pairs = [psum.tile([P, 2, last_width], F32, name=f"pair{u}", tag=f"bank{tags}{u}") for u in range(2)]
+                for t in range(PACK):
+                    for z in range(PASSES):
+                        multiply(pairs[t // 2][:, t % 2, :], z, t, last_first, last_width)
             bank_first = max(stretch[0] for stretch in STRETCHES if stretch[0] <= first)
             in_bank = first - bank_first
             summed = ring.tile([P, PACK, width], F32, name="summed")
-            for t in range(PACK):
-                nc.vector.tensor_tensor(
-                    summed[:, t, :], banks[bank_first, t][:, in_bank : in_bank + width], pos_of[first][:, t, :width], ADD
-                )
+            if bank_first == STRETCHES[2][0]:
+                for u in range(2):
+                    nc.vector.tensor_tensor(
+                        summed[:, 2 * u : 2 * u + 2, :],
+                        pairs[u][:, :, in_bank : in_bank + width],
+                        pos_of[first][:, 2 * u : 2 * u + 2, :width],
+                        ADD,
+                    )
+            else:
+                for t in range(PACK):
+                    nc.vector.tensor_tensor(
+                        summed[:, t, :], banks[bank_first, t][:, in_bank : in_bank + width], pos_of[first][:, t, :width], ADD
+                    )
             nc.scalar.activation(
                 hidden[:, PACK * first : PACK * (first + width)].rearrange("p (c n t) -> p c t n", n=4, t=PACK),
                 summed[:].rearrange("p t (c n) -> p c t n", n=4),
@@ -194,7 +211,7 @@ def tile_picked_phpq_gelu_p_kernel(
             nc.vector.quantize_mx(
                 out=h_codes[:].bitcast(FP8X4), scales=h_plane[:], in_=hidden[:, PACK * first : PACK * (first + width)]
             )
-            acc = psum.tile([P, width], F32, name="acc", tag=f"bank{1 - piece // PACK}{piece % PACK}")
+            acc = psum.tile([P, width], F32, name="acc", tag=OUT_BANKS[piece])
             nc.tensor.matmul_mx(
                 out=acc[:],
                 lhsT=w2_codes[:].bitcast(FP4X4),

@@ -22,17 +22,16 @@ K_PASS = P * PACK
 PASSES = K // K_PASS
 GROUP = 16
 QUADRANT = 32
-HALF = 512
-STRETCHES = ((0, 256, 0), (256, 512, 1), (768, 256, 0))
-OUT_BANKS = ("bank02", "bank03", "bank10", "bank11", "bank12")
-SCALAR_COLUMNS = 64
-TABLE_HEAD = 512
-POS_WIDTHS = (256, 256, 256, 256)
+TABLE_HEAD = 768
+QUARTER = S // 4
+LEAD, MIDDLE, LAST = (0, QUARTER), (QUARTER, 2 * QUARTER), (3 * QUARTER, QUARTER)
+SCALAR_SHARE_PASS0 = 96
+SCALAR_SHARE_PASS1 = 64
 GELU_WIDTHS = (128, 128, 128, 128, 128, 128, 128, 64, 64)
-GELU_BUFS = 5
-WIDE, NARROW = 256, 128
-OUT_WIDTHS = (WIDE, WIDE, WIDE, NARROW, NARROW)
-STORE_ENDS = (WIDE, 2 * WIDE, 3 * WIDE, 3 * WIDE + NARROW, S)
+RING_BUFS = 5
+OUT_WIDTHS = (256, 256, 256, 128, 128)
+OUT_BANKS = (2, 3, 4, 5, 6)
+SCALAR_PIECES = 2
 
 
 def tile_picked_phpq_gelu_p_kernel(
@@ -41,8 +40,8 @@ def tile_picked_phpq_gelu_p_kernel(
     nc = tc.nc
     with ExitStack() as ctx:
         keep = ctx.enter_context(tc.tile_pool(name="keep", bufs=1))
-        after = ctx.enter_context(tc.tile_pool(name="after", bufs=1))
-        ring = ctx.enter_context(tc.tile_pool(name="ring", bufs=GELU_BUFS))
+        placed = ctx.enter_context(tc.tile_pool(name="placed", bufs=1))
+        ring = ctx.enter_context(tc.tile_pool(name="ring", bufs=RING_BUFS))
         psum = ctx.enter_context(tc.psum_pool(name="psum", bufs=1))
 
         lists = keep.tile([P, S // GROUP], U16, name="lists")
@@ -51,16 +50,12 @@ def tile_picked_phpq_gelu_p_kernel(
         table_rows = [x_words[z].rearrange("p c r -> p (c r)").bitcast(I32) for z in range(PASSES)]
         nc.sync.dma_start(word_table[0][:, :TABLE_HEAD], table_rows[0][:, :TABLE_HEAD])
 
-        scale_table = after.tile([P, T], U8, name="scale_table", align_bytes=64, offset=0)
+        scale_table = placed.tile([P, T], U8, name="scale_table", align_bytes=64, offset=0)
         nc.vector.memset(scale_table[:].bitcast(I32), 0)
         for z in range(PASSES):
             rows = x_scales[z].rearrange("(g s) c -> s g c", s=2)
             for s in range(2):
                 nc.sync.dma_start(scale_table[4 * z + s : P : GROUP, :].bitcast(I32), rows[s].bitcast(I32))
-
-        warm = keep.tile([P, 16], F32, name="warm")
-        nc.vector.memset(warm[:, :8], 0.0)
-        nc.scalar.activation(warm[:, 8:], warm[:, :8], GELU)
 
         w1_rows = [w1[z * K_PASS : (z + 1) * K_PASS, :].rearrange("(p j) c -> p j c", j=PACK) for z in range(PASSES)]
         w1_first = keep.tile([P, PACK, H], F32, name="w1_first")
@@ -71,9 +66,9 @@ def tile_picked_phpq_gelu_p_kernel(
         picked_scales = keep.tile([P, S], U8, name="picked_scales", align_bytes=64)
         nc.vector.tensor_copy(picked_scales[:], scale_table[:].indirect(lists[:]))
 
-        late = after.tile([P, PACK * (H + S)], F32, name="late", align_bytes=64, offset=2 * N)
+        late = placed.tile([P, PACK * (H + S)], F32, name="late", align_bytes=64, offset=2 * N)
         w1_raw = [w1_first[:], late[:, : PACK * H].rearrange("p (j c) -> p j c", j=PACK)]
-        w2_codes = after.tile([P, 2 * N], U8, name="w2_codes", align_bytes=64, offset=0)
+        w2_codes = placed.tile([P, 2 * N], U8, name="w2_codes", align_bytes=64, offset=0)
         nc.sync.dma_start(w2_codes[:].bitcast(I32), w2_words[0].bitcast(I32))
 
         x_plane = keep.tile([P, S], U8, name="x_plane", align_bytes=64)
@@ -86,25 +81,16 @@ def tile_picked_phpq_gelu_p_kernel(
                 )
 
         nc.sync.dma_start(w1_raw[1], w1_rows[1])
+        pos_sb = late[:, PACK * H :].rearrange("p (g t c) -> p g t c", t=PACK, c=QUARTER)
         pos_rows = pos.rearrange("(p t) c -> p t c", t=PACK)
-        pos_of = {}
-        first = 0
-        for width in POS_WIDTHS:
-            part = late[:, PACK * (H + first) : PACK * (H + first + width)].rearrange("p (t c) -> p t c", t=PACK)
-            nc.sync.dma_start(part, pos_rows[:, :, first : first + width])
-            for column in range(0, width, 64):
-                pos_of[first + column] = part[:, :, column:]
-            first = first + width
+        for g in range(S // QUARTER):
+            nc.sync.dma_start(pos_sb[:, g], pos_rows[:, :, g * QUARTER : (g + 1) * QUARTER])
 
         picked, w1_codes, w1_plane = {}, {}, {}
 
-        def gather_words(z, first, width, tag):
-            words = keep.tile([P, width], U32, name=f"picked{z}{first}", tag=tag, align_bytes=64)
-            offsets = lists[:, first // GROUP : (first + width) // GROUP]
-            nc.vector.tensor_copy(words[:], word_table[z][:].bitcast(U32).indirect(offsets))
-            for start, columns, tags in STRETCHES:
-                if first <= start < first + width:
-                    picked[z, start] = words[:, start - first : start - first + columns]
+        def gather_words(z, tag):
+            picked[z] = keep.tile([P, S], U32, name=f"picked{z}", tag=tag, align_bytes=64)
+            nc.vector.tensor_copy(picked[z][:], word_table[z][:].bitcast(U32).indirect(lists[:]))
 
         grouped = {
             (z, u): keep.tile([P, 2 * H], BF16, name=f"w1_grouped{z}{u}", tag=f"grouped{z}{u}", align_bytes=64)
@@ -112,21 +98,21 @@ def tile_picked_phpq_gelu_p_kernel(
             for u in range(2)
         }
 
-        def cast_w1(engine_copy, z, u, columns):
+        def round_w1(engine_copy, z, u, columns):
             engine_copy(
                 grouped[z, u][:].rearrange("p (e m j) -> p m j e", e=2, j=PACK)[:, columns],
                 w1_raw[z].rearrange("p j (m u e) -> p u m j e", u=2, e=2)[:, u, columns],
             )
 
-        def quantize_w1(z, u, tag):
-            codes = keep.tile([P, 2 * P], U32, name=f"w1_codes{z}{u}", tag=tag, align_bytes=64)
+        def quantize_w1(z, u):
+            codes = keep.tile([P, 2 * P], U32, name=f"w1_codes{z}{u}", align_bytes=64)
             plane = keep.tile([P, 2 * P], U8, name=f"w1_plane{z}{u}", align_bytes=64)
             nc.vector.quantize_mx(out=codes[:].bitcast(FP8X4), scales=plane[:], in_=grouped[z, u][:])
             for e in range(2):
                 w1_codes[z, 2 * u + e] = codes[:, e * P : (e + 1) * P]
                 w1_plane[z, 2 * u + e] = plane[:, e * P : (e + 1) * P]
 
-        gather_words(0, 0, S, "picked0")
+        gather_words(0, "picked0")
 
         w2_plane = keep.tile([P, N], U8, name="w2_plane", tag="table0", align_bytes=64)
         nc.gpsimd.memset(w2_plane[:].bitcast(I32), 0)
@@ -135,67 +121,67 @@ def tile_picked_phpq_gelu_p_kernel(
                 w2_plane[QUADRANT * q : QUADRANT * q + 4, :].bitcast(I32), w2_scales[0, 4 * q : 4 * q + 4, :].bitcast(I32)
             )
 
-        cast_w1(nc.scalar.copy, 0, 0, slice(0, P))
-        cast_w1(nc.scalar.copy, 0, 1, slice(0, 3 * P // 4))
-        cast_w1(nc.vector.tensor_copy, 0, 1, slice(3 * P // 4, P))
+        round_w1(nc.scalar.copy, 0, 0, slice(0, P))
+        round_w1(nc.scalar.copy, 0, 1, slice(0, SCALAR_SHARE_PASS0))
+        round_w1(nc.vector.tensor_copy, 0, 1, slice(SCALAR_SHARE_PASS0, P))
         for u in range(2):
-            quantize_w1(0, u, f"codes0{u}")
-        gather_words(1, 0, S, "picked1")
+            quantize_w1(0, u)
+        gather_words(1, "grouped01")
         for u in range(2):
-            cast_w1(nc.scalar.copy, 1, u, slice(0, SCALAR_COLUMNS))
-            cast_w1(nc.vector.tensor_copy, 1, u, slice(SCALAR_COLUMNS, P))
+            round_w1(nc.scalar.copy, 1, u, slice(0, SCALAR_SHARE_PASS1))
+            round_w1(nc.vector.tensor_copy, 1, u, slice(SCALAR_SHARE_PASS1, P))
         for u in range(2):
-            quantize_w1(1, u, f"codes1{u}")
+            quantize_w1(1, u)
 
-        banks = {}
-
-        def multiply(acc, z, t, first, width):
+        def first_product(acc, z, t, stretch):
+            first, width = stretch
             nc.tensor.matmul_mx(
                 out=acc,
                 lhsT=w1_codes[z, t].bitcast(FP8X4),
                 lhsT_scale=w1_plane[z, t],
-                rhs=picked[z, first].bitcast(FP8X4),
+                rhs=picked[z][:, first : first + width].bitcast(FP8X4),
                 rhs_scale=x_plane[4 * z : P, first : first + width],
                 start=(z == 0),
                 stop=(z == PASSES - 1),
             )
 
-        def products(z, stretch):
-            first, width, tags = stretch
-            for t in range(PACK):
-                if z == 0:
-                    banks[first, t] = psum.tile([P, width], F32, name=f"bank{first}{t}", tag=f"bank{tags}{t}")
-                multiply(banks[first, t][:], z, t, first, width)
-
+        held = {
+            stretch: [
+                (psum.tile([P, 1, stretch[1]], F32, name=f"bank{bank0 + t}", tag=f"bank{bank0 + t}"), t, 1)
+                for t in range(PACK)
+            ]
+            for stretch, bank0 in ((LEAD, 0), (MIDDLE, PACK))
+        }
         for z in range(PASSES):
-            products(z, STRETCHES[0])
-            products(z, STRETCHES[1])
+            for stretch in (LEAD, MIDDLE):
+                for bank, t, count in held[stretch]:
+                    first_product(bank[:, 0, :], z, t, stretch)
+
+        def multiply_last_stretch():
+            held[LAST] = [
+                (psum.tile([P, 2, QUARTER], F32, name=f"pair{u}", tag=f"bank{u}"), 2 * u, 2) for u in range(2)
+            ]
+            for bank, t, count in held[LAST]:
+                for e in range(count):
+                    for z in range(PASSES):
+                        first_product(bank[:, e, :], z, t + e, LAST)
 
         hidden = keep.tile([P, PACK * S], BF16, name="hidden", align_bytes=64)
         first = 0
         for width in GELU_WIDTHS:
-            if first == STRETCHES[0][1]:
-                last_first, last_width, tags = STRETCHES[2]
-                pairs = [psum.tile([P, 2, last_width], F32, name=f"pair{u}", tag=f"bank{tags}{u}") for u in range(2)]
-                for t in range(PACK):
-                    for z in range(PASSES):
-                        multiply(pairs[t // 2][:, t % 2, :], z, t, last_first, last_width)
-            bank_first = max(stretch[0] for stretch in STRETCHES if stretch[0] <= first)
-            in_bank = first - bank_first
+            if first == MIDDLE[0]:
+                multiply_last_stretch()
+            stretch = max(s for s in (LEAD, MIDDLE, LAST) if s[0] <= first)
+            in_bank = first - stretch[0]
+            g, in_load = divmod(first, QUARTER)
             summed = ring.tile([P, PACK, width], F32, name="summed")
-            if bank_first == STRETCHES[2][0]:
-                for u in range(2):
-                    nc.vector.tensor_tensor(
-                        summed[:, 2 * u : 2 * u + 2, :],
-                        pairs[u][:, :, in_bank : in_bank + width],
-                        pos_of[first][:, 2 * u : 2 * u + 2, :width],
-                        ADD,
-                    )
-            else:
-                for t in range(PACK):
-                    nc.vector.tensor_tensor(
-                        summed[:, t, :], banks[bank_first, t][:, in_bank : in_bank + width], pos_of[first][:, t, :width], ADD
-                    )
+            for bank, t, count in held[stretch]:
+                nc.vector.tensor_tensor(
+                    summed[:, t : t + count, :],
+                    bank[:, :, in_bank : in_bank + width],
+                    pos_sb[:, g, t : t + count, in_load : in_load + width],
+                    ADD,
+                )
             nc.scalar.activation(
                 hidden[:, PACK * first : PACK * (first + width)].rearrange("p (c n t) -> p c t n", n=4, t=PACK),
                 summed[:].rearrange("p t (c n) -> p c t n", n=4),
@@ -203,15 +189,15 @@ def tile_picked_phpq_gelu_p_kernel(
             )
             first = first + width
 
-        products = []
+        pieces = []
         first = 0
-        for piece, width in enumerate(OUT_WIDTHS):
+        for width, out_bank in zip(OUT_WIDTHS, OUT_BANKS):
             h_codes = ring.tile([P, width], U32, name="h_codes", align_bytes=64)
             h_plane = ring.tile([P, width], U8, name="h_plane", align_bytes=64)
             nc.vector.quantize_mx(
                 out=h_codes[:].bitcast(FP8X4), scales=h_plane[:], in_=hidden[:, PACK * first : PACK * (first + width)]
             )
-            acc = psum.tile([P, width], F32, name="acc", tag=OUT_BANKS[piece])
+            acc = psum.tile([P, width], F32, name="acc", tag=f"bank{out_bank}")
             nc.tensor.matmul_mx(
                 out=acc[:],
                 lhsT=w2_codes[:].bitcast(FP4X4),
@@ -221,15 +207,11 @@ def tile_picked_phpq_gelu_p_kernel(
                 start=True,
                 stop=True,
             )
-            products.append((acc, first, width))
+            pieces.append((acc, slice(first, first + width)))
             first = first + width
 
         result = keep.tile([P, S], F32, name="result")
-        stored = 0
-        for acc, first, width in products:
-            end = first + width
-            engine_copy = nc.scalar.copy if end <= 2 * WIDE else nc.vector.tensor_copy
-            engine_copy(result[:, first:end], acc[:])
-            if end in STORE_ENDS:
-                nc.sync.dma_start(out[:, stored:end], result[:, stored:end])
-                stored = end
+        for piece, (acc, vectors) in enumerate(pieces):
+            engine_copy = nc.scalar.copy if piece < SCALAR_PIECES else nc.vector.tensor_copy
+            engine_copy(result[:, vectors], acc[:])
+            nc.sync.dma_start(out[:, vectors], result[:, vectors])

@@ -24,13 +24,14 @@ GROUP = 16
 QUADRANT = 32
 TABLE_HEAD = 768
 QUARTER = S // 4
-LEAD, MIDDLE, LAST = (0, QUARTER), (QUARTER, 2 * QUARTER), (3 * QUARTER, QUARTER)
+POS_WIDTHS = (256, 256, 256, 128, 128)
 SCALAR_SHARE_PASS0 = 96
-SCALAR_SHARE_PASS1 = 64
+SCALAR_SHARE_PASS1 = 48
 GELU_WIDTHS = (128, 128, 128, 128, 128, 128, 128, 64, 64)
 RING_BUFS = 5
 OUT_WIDTHS = (256, 256, 256, 128, 128)
 OUT_BANKS = (2, 3, 4, 5, 6)
+EARLY_PIECES_AT = (512, 896)
 SCALAR_PIECES = 2
 
 
@@ -44,18 +45,22 @@ def tile_picked_phpq_gelu_p_kernel(
         ring = ctx.enter_context(tc.tile_pool(name="ring", bufs=RING_BUFS))
         psum = ctx.enter_context(tc.psum_pool(name="psum", bufs=1))
 
-        lists = keep.tile([P, S // GROUP], U16, name="lists")
-        nc.sync.dma_start(lists[:], offs)
         word_table = [keep.tile([P, T], I32, name=f"word_table{z}", tag=f"table{z}", align_bytes=64) for z in range(PASSES)]
         table_rows = [x_words[z].rearrange("p c r -> p (c r)").bitcast(I32) for z in range(PASSES)]
         nc.sync.dma_start(word_table[0][:, :TABLE_HEAD], table_rows[0][:, :TABLE_HEAD])
+        lists = keep.tile([P, S // GROUP], U16, name="lists")
+        nc.sync.dma_start(lists[:], offs)
 
-        scale_table = placed.tile([P, T], U8, name="scale_table", align_bytes=64, offset=0)
+        scale_table = keep.tile([P, T], U8, name="scale_table", align_bytes=64)
         nc.vector.memset(scale_table[:].bitcast(I32), 0)
         for z in range(PASSES):
             rows = x_scales[z].rearrange("(g s) c -> s g c", s=2)
             for s in range(2):
                 nc.sync.dma_start(scale_table[4 * z + s : P : GROUP, :].bitcast(I32), rows[s].bitcast(I32))
+
+        unread_gelu = keep.tile([P, 16], F32, name="unread_gelu")
+        nc.gpsimd.memset(unread_gelu[:, 0:1], 0.0)
+        nc.scalar.activation(unread_gelu[:, 8:9], unread_gelu[:, 0:1], GELU)
 
         w1_rows = [w1[z * K_PASS : (z + 1) * K_PASS, :].rearrange("(p j) c -> p j c", j=PACK) for z in range(PASSES)]
         w1_first = keep.tile([P, PACK, H], F32, name="w1_first")
@@ -63,13 +68,11 @@ def tile_picked_phpq_gelu_p_kernel(
         nc.sync.dma_start(w1_first[:], w1_rows[0])
         nc.sync.dma_start(word_table[1][:], table_rows[1])
 
-        picked_scales = keep.tile([P, S], U8, name="picked_scales", align_bytes=64)
+        picked_scales = placed.tile([P, S], U8, name="picked_scales", align_bytes=64, offset=0)
         nc.vector.tensor_copy(picked_scales[:], scale_table[:].indirect(lists[:]))
 
-        late = placed.tile([P, PACK * (H + S)], F32, name="late", align_bytes=64, offset=2 * N)
+        late = placed.tile([P, PACK * (H + S)], F32, name="late", align_bytes=64, offset=0)
         w1_raw = [w1_first[:], late[:, : PACK * H].rearrange("p (j c) -> p j c", j=PACK)]
-        w2_codes = placed.tile([P, 2 * N], U8, name="w2_codes", align_bytes=64, offset=0)
-        nc.sync.dma_start(w2_codes[:].bitcast(I32), w2_words[0].bitcast(I32))
 
         x_plane = keep.tile([P, S], U8, name="x_plane", align_bytes=64)
         nc.vector.tensor_copy(x_plane[:].bitcast(I32), picked_scales[:].bitcast(I32))
@@ -77,14 +80,18 @@ def tile_picked_phpq_gelu_p_kernel(
             for s in range(2):
                 nc.sync.dma_start(
                     x_plane[4 * z + 2 + s : P : QUADRANT, :].bitcast(I32),
-                    picked_scales[GROUP + 4 * z + s : P : QUADRANT, :].bitcast(I32),
+                    x_plane[GROUP + 4 * z + s : P : QUADRANT, :].bitcast(I32),
                 )
 
         nc.sync.dma_start(w1_raw[1], w1_rows[1])
-        pos_sb = late[:, PACK * H :].rearrange("p (g t c) -> p g t c", t=PACK, c=QUARTER)
         pos_rows = pos.rearrange("(p t) c -> p t c", t=PACK)
-        for g in range(S // QUARTER):
-            nc.sync.dma_start(pos_sb[:, g], pos_rows[:, :, g * QUARTER : (g + 1) * QUARTER])
+        pos_loads = []
+        first = 0
+        for width in POS_WIDTHS:
+            load = late[:, PACK * (H + first) : PACK * (H + first + width)].rearrange("p (t c) -> p t c", t=PACK)
+            nc.sync.dma_start(load, pos_rows[:, :, first : first + width])
+            pos_loads.append((first, load))
+            first = first + width
 
         picked, w1_codes, w1_plane = {}, {}, {}
 
@@ -104,15 +111,28 @@ def tile_picked_phpq_gelu_p_kernel(
                 w1_raw[z].rearrange("p j (m u e) -> p u m j e", u=2, e=2)[:, u, columns],
             )
 
-        def quantize_w1(z, u):
+        def quantize_w1(z, u, calls):
             codes = keep.tile([P, 2 * P], U32, name=f"w1_codes{z}{u}", align_bytes=64)
             plane = keep.tile([P, 2 * P], U8, name=f"w1_plane{z}{u}", align_bytes=64)
-            nc.vector.quantize_mx(out=codes[:].bitcast(FP8X4), scales=plane[:], in_=grouped[z, u][:])
+            step = 2 * P // calls
+            for c in range(0, 2 * P, step):
+                nc.vector.quantize_mx(
+                    out=codes[:, c : c + step].bitcast(FP8X4),
+                    scales=plane[:, c : c + step],
+                    in_=grouped[z, u][:, PACK * c : PACK * (c + step)],
+                )
             for e in range(2):
                 w1_codes[z, 2 * u + e] = codes[:, e * P : (e + 1) * P]
                 w1_plane[z, 2 * u + e] = plane[:, e * P : (e + 1) * P]
 
         gather_words(0, "picked0")
+
+        round_w1(nc.scalar.copy, 0, 0, slice(0, P))
+        round_w1(nc.scalar.copy, 0, 1, slice(0, SCALAR_SHARE_PASS0))
+        round_w1(nc.vector.tensor_copy, 0, 1, slice(SCALAR_SHARE_PASS0, P))
+        for u in range(2):
+            quantize_w1(0, u, 1)
+        gather_words(1, "grouped01")
 
         w2_plane = keep.tile([P, N], U8, name="w2_plane", tag="table0", align_bytes=64)
         nc.gpsimd.memset(w2_plane[:].bitcast(I32), 0)
@@ -120,18 +140,14 @@ def tile_picked_phpq_gelu_p_kernel(
             nc.sync.dma_start(
                 w2_plane[QUADRANT * q : QUADRANT * q + 4, :].bitcast(I32), w2_scales[0, 4 * q : 4 * q + 4, :].bitcast(I32)
             )
+        w2_codes = keep.tile([P, 2 * N], U8, name="w2_codes", tag="grouped00", align_bytes=64)
+        nc.sync.dma_start(w2_codes[:].bitcast(I32), w2_words[0].bitcast(I32))
 
-        round_w1(nc.scalar.copy, 0, 0, slice(0, P))
-        round_w1(nc.scalar.copy, 0, 1, slice(0, SCALAR_SHARE_PASS0))
-        round_w1(nc.vector.tensor_copy, 0, 1, slice(SCALAR_SHARE_PASS0, P))
-        for u in range(2):
-            quantize_w1(0, u)
-        gather_words(1, "grouped01")
         for u in range(2):
             round_w1(nc.scalar.copy, 1, u, slice(0, SCALAR_SHARE_PASS1))
             round_w1(nc.vector.tensor_copy, 1, u, slice(SCALAR_SHARE_PASS1, P))
         for u in range(2):
-            quantize_w1(1, u)
+            quantize_w1(1, u, 2)
 
         def first_product(acc, z, t, stretch):
             first, width = stretch
@@ -145,59 +161,44 @@ def tile_picked_phpq_gelu_p_kernel(
                 stop=(z == PASSES - 1),
             )
 
-        held = {
-            stretch: [
-                (psum.tile([P, 1, stretch[1]], F32, name=f"bank{bank0 + t}", tag=f"bank{bank0 + t}"), t, 1)
-                for t in range(PACK)
+        def banks(g, bank0, count):
+            held[g] = [
+                (psum.tile([P, count, QUARTER], F32, name=f"bank{g}{t}", tag=f"bank{bank0 + t // count}"), t, count)
+                for t in range(0, PACK, count)
             ]
-            for stretch, bank0 in ((LEAD, 0), (MIDDLE, PACK))
-        }
-        for z in range(PASSES):
-            for stretch in (LEAD, MIDDLE):
-                for bank, t, count in held[stretch]:
-                    first_product(bank[:, 0, :], z, t, stretch)
 
-        def multiply_last_stretch():
-            held[LAST] = [
-                (psum.tile([P, 2, QUARTER], F32, name=f"pair{u}", tag=f"bank{u}"), 2 * u, 2) for u in range(2)
-            ]
-            for bank, t, count in held[LAST]:
+        held = {}
+        banks(0, 0, 1)
+        banks(1, 4, 2)
+        banks(2, 6, 2)
+        for g in range(3):
+            for bank, t, count in held[g]:
+                first_product(bank[:, 0, :], 0, t, (g * QUARTER, QUARTER))
+        for g in range(3):
+            for bank, t, count in held[g]:
+                first_product(bank[:, 0, :], 1, t, (g * QUARTER, QUARTER))
+                for e in range(1, count):
+                    for z in range(PASSES):
+                        first_product(bank[:, e, :], z, t + e, (g * QUARTER, QUARTER))
+
+        def multiply_last_quarter():
+            banks(3, 0, 2)
+            for bank, t, count in held[3]:
                 for e in range(count):
                     for z in range(PASSES):
-                        first_product(bank[:, e, :], z, t + e, LAST)
+                        first_product(bank[:, e, :], z, t + e, (3 * QUARTER, QUARTER))
 
         hidden = keep.tile([P, PACK * S], BF16, name="hidden", align_bytes=64)
-        first = 0
-        for width in GELU_WIDTHS:
-            if first == MIDDLE[0]:
-                multiply_last_stretch()
-            stretch = max(s for s in (LEAD, MIDDLE, LAST) if s[0] <= first)
-            in_bank = first - stretch[0]
-            g, in_load = divmod(first, QUARTER)
-            summed = ring.tile([P, PACK, width], F32, name="summed")
-            for bank, t, count in held[stretch]:
-                nc.vector.tensor_tensor(
-                    summed[:, t : t + count, :],
-                    bank[:, :, in_bank : in_bank + width],
-                    pos_sb[:, g, t : t + count, in_load : in_load + width],
-                    ADD,
-                )
-            nc.scalar.activation(
-                hidden[:, PACK * first : PACK * (first + width)].rearrange("p (c n t) -> p c t n", n=4, t=PACK),
-                summed[:].rearrange("p t (c n) -> p c t n", n=4),
-                GELU,
-            )
-            first = first + width
-
         pieces = []
-        first = 0
-        for width, out_bank in zip(OUT_WIDTHS, OUT_BANKS):
+
+        def second_product():
+            first, width = sum(OUT_WIDTHS[: len(pieces)]), OUT_WIDTHS[len(pieces)]
             h_codes = ring.tile([P, width], U32, name="h_codes", align_bytes=64)
             h_plane = ring.tile([P, width], U8, name="h_plane", align_bytes=64)
             nc.vector.quantize_mx(
                 out=h_codes[:].bitcast(FP8X4), scales=h_plane[:], in_=hidden[:, PACK * first : PACK * (first + width)]
             )
-            acc = psum.tile([P, width], F32, name="acc", tag=f"bank{out_bank}")
+            acc = psum.tile([P, width], F32, name="acc", tag=f"bank{OUT_BANKS[len(pieces)]}")
             nc.tensor.matmul_mx(
                 out=acc[:],
                 lhsT=w2_codes[:].bitcast(FP4X4),
@@ -208,7 +209,32 @@ def tile_picked_phpq_gelu_p_kernel(
                 stop=True,
             )
             pieces.append((acc, slice(first, first + width)))
+
+        first = 0
+        for width in GELU_WIDTHS:
+            if first == QUARTER:
+                multiply_last_quarter()
+            if first in EARLY_PIECES_AT:
+                second_product()
+            g, in_bank = divmod(first, QUARTER)
+            load_first, load = [entry for entry in pos_loads if entry[0] <= first][-1]
+            in_load = first - load_first
+            summed = ring.tile([P, PACK, width], F32, name="summed")
+            for bank, t, count in held[g]:
+                nc.vector.tensor_tensor(
+                    summed[:, t : t + count, :],
+                    bank[:, :, in_bank : in_bank + width],
+                    load[:, t : t + count, in_load : in_load + width],
+                    ADD,
+                )
+            nc.scalar.activation(
+                hidden[:, PACK * first : PACK * (first + width)].rearrange("p (c n t) -> p c t n", n=4, t=PACK),
+                summed[:].rearrange("p t (c n) -> p c t n", n=4),
+                GELU,
+            )
             first = first + width
+        for rest in range(len(OUT_WIDTHS) - len(EARLY_PIECES_AT)):
+            second_product()
 
         result = keep.tile([P, S], F32, name="result")
         for piece, (acc, vectors) in enumerate(pieces):

@@ -24,14 +24,15 @@ GROUP = 16
 QUADRANT = 32
 TABLE_HEAD = 768
 QUARTER = S // 4
+LEAD, MIDDLE, LAST = (0, QUARTER), (QUARTER, 2 * QUARTER), (3 * QUARTER, QUARTER)
 POS_WIDTHS = (256, 256, 256, 128, 128)
 SCALAR_SHARE_PASS0 = 96
-SCALAR_SHARE_PASS1 = 48
+SCALAR_SHARE_PASS1 = 56
 GELU_WIDTHS = (128, 128, 128, 128, 128, 128, 128, 64, 64)
 RING_BUFS = 5
 OUT_WIDTHS = (256, 256, 256, 128, 128)
 OUT_BANKS = (2, 3, 4, 5, 6)
-EARLY_PIECES_AT = (512, 896)
+EARLY_PIECES_AT = (768,)
 SCALAR_PIECES = 2
 
 
@@ -161,32 +162,26 @@ def tile_picked_phpq_gelu_p_kernel(
                 stop=(z == PASSES - 1),
             )
 
-        def banks(g, bank0, count):
-            held[g] = [
-                (psum.tile([P, count, QUARTER], F32, name=f"bank{g}{t}", tag=f"bank{bank0 + t // count}"), t, count)
-                for t in range(0, PACK, count)
+        held = {
+            stretch: [
+                (psum.tile([P, 1, stretch[1]], F32, name=f"bank{bank0 + t}", tag=f"bank{bank0 + t}"), t, 1)
+                for t in range(PACK)
             ]
+            for stretch, bank0 in ((LEAD, 0), (MIDDLE, PACK))
+        }
+        for z in range(PASSES):
+            for stretch in (LEAD, MIDDLE):
+                for bank, t, count in held[stretch]:
+                    first_product(bank[:, 0, :], z, t, stretch)
 
-        held = {}
-        banks(0, 0, 1)
-        banks(1, 4, 2)
-        banks(2, 6, 2)
-        for g in range(3):
-            for bank, t, count in held[g]:
-                first_product(bank[:, 0, :], 0, t, (g * QUARTER, QUARTER))
-        for g in range(3):
-            for bank, t, count in held[g]:
-                first_product(bank[:, 0, :], 1, t, (g * QUARTER, QUARTER))
-                for e in range(1, count):
-                    for z in range(PASSES):
-                        first_product(bank[:, e, :], z, t + e, (g * QUARTER, QUARTER))
-
-        def multiply_last_quarter():
-            banks(3, 0, 2)
-            for bank, t, count in held[3]:
+        def multiply_last_stretch():
+            held[LAST] = [
+                (psum.tile([P, 2, QUARTER], F32, name=f"pair{u}", tag=f"bank{u}"), 2 * u, 2) for u in range(2)
+            ]
+            for bank, t, count in held[LAST]:
                 for e in range(count):
                     for z in range(PASSES):
-                        first_product(bank[:, e, :], z, t + e, (3 * QUARTER, QUARTER))
+                        first_product(bank[:, e, :], z, t + e, LAST)
 
         hidden = keep.tile([P, PACK * S], BF16, name="hidden", align_bytes=64)
         pieces = []
@@ -212,15 +207,16 @@ def tile_picked_phpq_gelu_p_kernel(
 
         first = 0
         for width in GELU_WIDTHS:
-            if first == QUARTER:
-                multiply_last_quarter()
+            if first == MIDDLE[0]:
+                multiply_last_stretch()
             if first in EARLY_PIECES_AT:
                 second_product()
-            g, in_bank = divmod(first, QUARTER)
+            stretch = max(s for s in (LEAD, MIDDLE, LAST) if s[0] <= first)
+            in_bank = first - stretch[0]
             load_first, load = [entry for entry in pos_loads if entry[0] <= first][-1]
             in_load = first - load_first
             summed = ring.tile([P, PACK, width], F32, name="summed")
-            for bank, t, count in held[g]:
+            for bank, t, count in held[stretch]:
                 nc.vector.tensor_tensor(
                     summed[:, t : t + count, :],
                     bank[:, :, in_bank : in_bank + width],

@@ -21,19 +21,20 @@ PACK = 4
 K_PASS = P * PACK
 PASSES = K // K_PASS
 GROUP = 16
+BLOCK = 8
 QUADRANT = 32
 TABLE_HEAD = 768
 QUARTER = S // 4
 LEAD, MIDDLE, LAST = (0, QUARTER), (QUARTER, 2 * QUARTER), (3 * QUARTER, QUARTER)
-POS_WIDTHS = (256, 256, 256, 128, 128)
-SCALAR_SHARE_PASS0 = 96
+POS_WIDTHS = (256, 256, 256, 256)
+SCALAR_SHARE_PASS0 = 48
 SCALAR_SHARE_PASS1 = 56
 GELU_WIDTHS = (128, 128, 128, 128, 128, 128, 128, 64, 64)
 RING_BUFS = 5
 OUT_WIDTHS = (256, 256, 256, 128, 128)
 OUT_BANKS = (2, 3, 4, 5, 6)
-EARLY_PIECES_AT = (768,)
-SCALAR_PIECES = 2
+EARLY_PIECES_AT = ()
+SCALAR_PIECES = 3
 
 
 def tile_picked_phpq_gelu_p_kernel(
@@ -52,12 +53,13 @@ def tile_picked_phpq_gelu_p_kernel(
         lists = keep.tile([P, S // GROUP], U16, name="lists")
         nc.sync.dma_start(lists[:], offs)
 
-        scale_table = keep.tile([P, T], U8, name="scale_table", align_bytes=64)
+        scale_table = placed.tile([P, T], U8, name="scale_table", align_bytes=64, offset=0)
         nc.vector.memset(scale_table[:].bitcast(I32), 0)
         for z in range(PASSES):
-            rows = x_scales[z].rearrange("(g s) c -> s g c", s=2)
-            for s in range(2):
-                nc.sync.dma_start(scale_table[4 * z + s : P : GROUP, :].bitcast(I32), rows[s].bitcast(I32))
+            nc.sync.dma_start(scale_table[4 * z : P : BLOCK, :].bitcast(I32), x_scales[z].bitcast(I32))
+        x_plane = [keep.tile([P, S], U8, name=f"x_plane{z}", align_bytes=64) for z in range(PASSES)]
+        for z in range(PASSES):
+            nc.vector.memset(x_plane[z][:].bitcast(I32), 0)
 
         unread_gelu = keep.tile([P, 16], F32, name="unread_gelu")
         nc.gpsimd.memset(unread_gelu[:, 0:1], 0.0)
@@ -69,22 +71,22 @@ def tile_picked_phpq_gelu_p_kernel(
         nc.sync.dma_start(w1_first[:], w1_rows[0])
         nc.sync.dma_start(word_table[1][:], table_rows[1])
 
-        picked_scales = placed.tile([P, S], U8, name="picked_scales", align_bytes=64, offset=0)
+        picked_scales = keep.tile([P, S], U8, name="picked_scales", align_bytes=64)
         nc.vector.tensor_copy(picked_scales[:], scale_table[:].indirect(lists[:]))
 
         late = placed.tile([P, PACK * (H + S)], F32, name="late", align_bytes=64, offset=0)
         w1_raw = [w1_first[:], late[:, : PACK * H].rearrange("p (j c) -> p j c", j=PACK)]
 
-        x_plane = keep.tile([P, S], U8, name="x_plane", align_bytes=64)
-        nc.vector.tensor_copy(x_plane[:].bitcast(I32), picked_scales[:].bitcast(I32))
-        for z in range(PASSES):
-            for s in range(2):
+        def move_scale_rows(z):
+            for r in range(QUADRANT // BLOCK):
                 nc.sync.dma_start(
-                    x_plane[4 * z + 2 + s : P : QUADRANT, :].bitcast(I32),
-                    x_plane[GROUP + 4 * z + s : P : QUADRANT, :].bitcast(I32),
+                    x_plane[z][r:P:QUADRANT, :].bitcast(I32),
+                    picked_scales[BLOCK * r + 4 * z : P : QUADRANT, :].bitcast(I32),
                 )
 
+        move_scale_rows(0)
         nc.sync.dma_start(w1_raw[1], w1_rows[1])
+        move_scale_rows(1)
         pos_rows = pos.rearrange("(p t) c -> p t c", t=PACK)
         pos_loads = []
         first = 0
@@ -157,7 +159,7 @@ def tile_picked_phpq_gelu_p_kernel(
                 lhsT=w1_codes[z, t].bitcast(FP8X4),
                 lhsT_scale=w1_plane[z, t],
                 rhs=picked[z][:, first : first + width].bitcast(FP8X4),
-                rhs_scale=x_plane[4 * z : P, first : first + width],
+                rhs_scale=x_plane[z][:, first : first + width],
                 start=(z == 0),
                 stop=(z == PASSES - 1),
             )
@@ -224,8 +226,8 @@ def tile_picked_phpq_gelu_p_kernel(
                     ADD,
                 )
             nc.scalar.activation(
-                hidden[:, PACK * first : PACK * (first + width)].rearrange("p (c n t) -> p c t n", n=4, t=PACK),
-                summed[:].rearrange("p t (c n) -> p c t n", n=4),
+                hidden[:, PACK * first : PACK * (first + width)].rearrange("p (c n t) -> p c t n", n=2, t=PACK),
+                summed[:].rearrange("p t (c n) -> p c t n", n=2),
                 GELU,
             )
             first = first + width

@@ -33,7 +33,7 @@ GELU_WIDTHS = (128, 128, 128, 128, 128, 128, 128, 64, 64)
 RING_BUFS = 5
 OUT_WIDTHS = (256, 256, 256, 128, 128)
 OUT_BANKS = (2, 3, 4, 5, 6)
-EARLY_PIECES_AT = ()
+EARLY_PIECES_AT = (896,)
 SCALAR_PIECES = 3
 
 
@@ -187,10 +187,13 @@ def tile_picked_phpq_gelu_p_kernel(
 
         hidden = keep.tile([P, PACK * S], BF16, name="hidden", align_bytes=64)
         pieces = []
+        sums_at = 4 * PACK * (H + S)
+        sum_bytes = 4 * PACK * max(GELU_WIDTHS)
 
         def second_product():
             first, width = sum(OUT_WIDTHS[: len(pieces)]), OUT_WIDTHS[len(pieces)]
-            h_codes = ring.tile([P, width], U32, name="h_codes", align_bytes=64)
+            codes_at = sums_at + 4 * sum_bytes if not pieces else 4 * (PACK * H + first)
+            h_codes = placed.tile([P, width], U32, name=f"h_codes{first}", align_bytes=64, offset=codes_at)
             h_plane = ring.tile([P, width], U8, name="h_plane", align_bytes=64)
             nc.vector.quantize_mx(
                 out=h_codes[:].bitcast(FP8X4), scales=h_plane[:], in_=hidden[:, PACK * first : PACK * (first + width)]
@@ -208,7 +211,7 @@ def tile_picked_phpq_gelu_p_kernel(
             pieces.append((acc, slice(first, first + width)))
 
         first = 0
-        for width in GELU_WIDTHS:
+        for piece, width in enumerate(GELU_WIDTHS):
             if first == MIDDLE[0]:
                 multiply_last_stretch()
             if first in EARLY_PIECES_AT:
@@ -217,7 +220,9 @@ def tile_picked_phpq_gelu_p_kernel(
             in_bank = first - stretch[0]
             load_first, load = [entry for entry in pos_loads if entry[0] <= first][-1]
             in_load = first - load_first
-            summed = ring.tile([P, PACK, width], F32, name="summed")
+            summed = placed.tile(
+                [P, PACK, width], F32, name=f"summed{piece}", align_bytes=64, offset=sums_at + piece % RING_BUFS * sum_bytes
+            )
             for bank, t, count in held[stretch]:
                 nc.vector.tensor_tensor(
                     summed[:, t : t + count, :],

@@ -61,10 +61,6 @@ def tile_picked_phpq_gelu_p_kernel(
         for z in range(PASSES):
             nc.vector.memset(x_plane[z][:].bitcast(I32), 0)
 
-        unread_gelu = keep.tile([P, 16], F32, name="unread_gelu")
-        nc.gpsimd.memset(unread_gelu[:, 0:1], 0.0)
-        nc.scalar.activation(unread_gelu[:, 8:9], unread_gelu[:, 0:1], GELU)
-
         w1_rows = [w1[z * K_PASS : (z + 1) * K_PASS, :].rearrange("(p j) c -> p j c", j=PACK) for z in range(PASSES)]
         w1_first = keep.tile([P, PACK, H], F32, name="w1_first")
         nc.sync.dma_start(word_table[0][:, TABLE_HEAD:], table_rows[0][:, TABLE_HEAD:])

@@ -26,15 +26,18 @@ QUADRANT = 32
 TABLE_HEAD = 768
 QUARTER = S // 4
 LEAD, MIDDLE, LAST = (0, QUARTER), (QUARTER, 2 * QUARTER), (3 * QUARTER, QUARTER)
-POS_WIDTHS = (256, 256, 256, 256)
 SCALAR_SHARE_PASS0 = 48
 SCALAR_SHARE_PASS1 = 56
 GELU_WIDTHS = (128, 128, 128, 128, 128, 128, 128, 64, 64)
-RING_BUFS = 5
+SUM_SLOTS = 5
 OUT_WIDTHS = (256, 256, 256, 128, 128)
 OUT_BANKS = (2, 3, 4, 5, 6)
-EARLY_PIECES_AT = (896,)
-SCALAR_PIECES = 3
+EARLY_PIECE_AT = 512
+SCALAR_PIECES = 2
+LATE_AT = 0
+SUMS_AT = LATE_AT + 4 * PACK * (H + LAST[0])
+SUM_BYTES = 4 * PACK * max(GELU_WIDTHS)
+W1_FIRST_AT = SUMS_AT + SUM_SLOTS * SUM_BYTES
 
 
 def tile_picked_phpq_gelu_p_kernel(
@@ -44,16 +47,15 @@ def tile_picked_phpq_gelu_p_kernel(
     with ExitStack() as ctx:
         keep = ctx.enter_context(tc.tile_pool(name="keep", bufs=1))
         placed = ctx.enter_context(tc.tile_pool(name="placed", bufs=1))
-        ring = ctx.enter_context(tc.tile_pool(name="ring", bufs=RING_BUFS))
         psum = ctx.enter_context(tc.psum_pool(name="psum", bufs=1))
 
-        word_table = [keep.tile([P, T], I32, name=f"word_table{z}", tag=f"table{z}", align_bytes=64) for z in range(PASSES)]
+        word_table = [keep.tile([P, T], I32, name=f"word_table{z}", align_bytes=64) for z in range(PASSES)]
         table_rows = [x_words[z].rearrange("p c r -> p (c r)").bitcast(I32) for z in range(PASSES)]
         nc.sync.dma_start(word_table[0][:, :TABLE_HEAD], table_rows[0][:, :TABLE_HEAD])
         lists = keep.tile([P, S // GROUP], U16, name="lists")
         nc.sync.dma_start(lists[:], offs)
 
-        scale_table = placed.tile([P, T], U8, name="scale_table", align_bytes=64, offset=0)
+        scale_table = placed.tile([P, T], U8, name="scale_table", align_bytes=64, offset=LATE_AT)
         nc.vector.memset(scale_table[:].bitcast(I32), 0)
         for z in range(PASSES):
             nc.sync.dma_start(scale_table[4 * z : P : BLOCK, :].bitcast(I32), x_scales[z].bitcast(I32))
@@ -62,7 +64,7 @@ def tile_picked_phpq_gelu_p_kernel(
             nc.vector.memset(x_plane[z][:].bitcast(I32), 0)
 
         w1_rows = [w1[z * K_PASS : (z + 1) * K_PASS, :].rearrange("(p j) c -> p j c", j=PACK) for z in range(PASSES)]
-        w1_first = keep.tile([P, PACK, H], F32, name="w1_first")
+        w1_first = placed.tile([P, PACK, H], F32, name="w1_first", align_bytes=64, offset=W1_FIRST_AT)
         nc.sync.dma_start(word_table[0][:, TABLE_HEAD:], table_rows[0][:, TABLE_HEAD:])
         nc.sync.dma_start(w1_first[:], w1_rows[0])
         nc.sync.dma_start(word_table[1][:], table_rows[1])
@@ -70,7 +72,7 @@ def tile_picked_phpq_gelu_p_kernel(
         picked_scales = keep.tile([P, S], U8, name="picked_scales", align_bytes=64)
         nc.vector.tensor_copy(picked_scales[:], scale_table[:].indirect(lists[:]))
 
-        late = placed.tile([P, PACK * (H + S)], F32, name="late", align_bytes=64, offset=0)
+        late = placed.tile([P, PACK * (H + LAST[0])], F32, name="late", align_bytes=64, offset=LATE_AT)
         w1_raw = [w1_first[:], late[:, : PACK * H].rearrange("p (j c) -> p j c", j=PACK)]
 
         def move_scale_rows(z):
@@ -84,18 +86,19 @@ def tile_picked_phpq_gelu_p_kernel(
         nc.sync.dma_start(w1_raw[1], w1_rows[1])
         move_scale_rows(1)
         pos_rows = pos.rearrange("(p t) c -> p t c", t=PACK)
-        pos_loads = []
-        first = 0
-        for width in POS_WIDTHS:
-            load = late[:, PACK * (H + first) : PACK * (H + first + width)].rearrange("p (t c) -> p t c", t=PACK)
-            nc.sync.dma_start(load, pos_rows[:, :, first : first + width])
-            pos_loads.append((first, load))
-            first = first + width
+        pos_quarter = []
+        for first in range(0, LAST[0], QUARTER):
+            load = late[:, PACK * (H + first) : PACK * (H + first + QUARTER)].rearrange("p (t c) -> p t c", t=PACK)
+            nc.sync.dma_start(load, pos_rows[:, :, first : first + QUARTER])
+            pos_quarter.append(load)
 
-        picked, w1_codes, w1_plane = {}, {}, {}
+        picked = [
+            keep.tile([P, S], U32, name="picked0", align_bytes=64),
+            placed.tile([P, S], U32, name="picked1", align_bytes=64, offset=W1_FIRST_AT + 4 * PACK * QUARTER),
+        ]
+        w1_codes, w1_plane = {}, {}
 
-        def gather_words(z, tag):
-            picked[z] = keep.tile([P, S], U32, name=f"picked{z}", tag=tag, align_bytes=64)
+        def gather_words(z):
             nc.vector.tensor_copy(picked[z][:], word_table[z][:].bitcast(U32).indirect(lists[:]))
 
         grouped = {
@@ -124,16 +127,22 @@ def tile_picked_phpq_gelu_p_kernel(
                 w1_codes[z, 2 * u + e] = codes[:, e * P : (e + 1) * P]
                 w1_plane[z, 2 * u + e] = plane[:, e * P : (e + 1) * P]
 
-        gather_words(0, "picked0")
-
+        gather_words(0)
         round_w1(nc.scalar.copy, 0, 0, slice(0, P))
         round_w1(nc.scalar.copy, 0, 1, slice(0, SCALAR_SHARE_PASS0))
         round_w1(nc.vector.tensor_copy, 0, 1, slice(SCALAR_SHARE_PASS0, P))
         for u in range(2):
             quantize_w1(0, u, 1)
-        gather_words(1, "grouped01")
+        gather_words(1)
 
-        w2_plane = keep.tile([P, N], U8, name="w2_plane", tag="table0", align_bytes=64)
+        pos_last = [
+            placed.tile([P, 2, QUARTER], F32, name=f"pos_last{u}", align_bytes=64, offset=W1_FIRST_AT + u * 4 * 2 * QUARTER)
+            for u in range(2)
+        ]
+        for u in range(2):
+            nc.sync.dma_start(pos_last[u][:], pos_rows[:, 2 * u : 2 * u + 2, LAST[0] :])
+
+        w2_plane = keep.tile([P, N], U8, name="w2_plane", tag="grouped01", align_bytes=64)
         nc.gpsimd.memset(w2_plane[:].bitcast(I32), 0)
         for q in range(P // QUADRANT):
             nc.sync.dma_start(
@@ -183,14 +192,15 @@ def tile_picked_phpq_gelu_p_kernel(
 
         hidden = keep.tile([P, PACK * S], BF16, name="hidden", align_bytes=64)
         pieces = []
-        sums_at = 4 * PACK * (H + S)
-        sum_bytes = 4 * PACK * max(GELU_WIDTHS)
 
         def second_product():
             first, width = sum(OUT_WIDTHS[: len(pieces)]), OUT_WIDTHS[len(pieces)]
-            codes_at = sums_at + 4 * sum_bytes if not pieces else 4 * (PACK * H + first)
-            h_codes = placed.tile([P, width], U32, name=f"h_codes{first}", align_bytes=64, offset=codes_at)
-            h_plane = ring.tile([P, width], U8, name="h_plane", align_bytes=64)
+            if pieces:
+                codes_at = W1_FIRST_AT + 4 * (first - OUT_WIDTHS[0])
+                h_codes = placed.tile([P, width], U32, name=f"h_codes{first}", align_bytes=64, offset=codes_at)
+            else:
+                h_codes = keep.tile([P, width], U32, name=f"h_codes{first}", align_bytes=64)
+            h_plane = keep.tile([P, width], U8, name=f"h_plane{first}", align_bytes=64)
             nc.vector.quantize_mx(
                 out=h_codes[:].bitcast(FP8X4), scales=h_plane[:], in_=hidden[:, PACK * first : PACK * (first + width)]
             )
@@ -210,20 +220,20 @@ def tile_picked_phpq_gelu_p_kernel(
         for piece, width in enumerate(GELU_WIDTHS):
             if first == MIDDLE[0]:
                 multiply_last_stretch()
-            if first in EARLY_PIECES_AT:
+            if first == EARLY_PIECE_AT:
                 second_product()
             stretch = max(s for s in (LEAD, MIDDLE, LAST) if s[0] <= first)
             in_bank = first - stretch[0]
-            load_first, load = [entry for entry in pos_loads if entry[0] <= first][-1]
-            in_load = first - load_first
+            quarter, in_quarter = divmod(first, QUARTER)
             summed = placed.tile(
-                [P, PACK, width], F32, name=f"summed{piece}", align_bytes=64, offset=sums_at + piece % RING_BUFS * sum_bytes
+                [P, PACK, width], F32, name=f"summed{piece}", align_bytes=64, offset=SUMS_AT + piece % SUM_SLOTS * SUM_BYTES
             )
             for bank, t, count in held[stretch]:
+                pos_here = pos_last[t // 2][:] if stretch == LAST else pos_quarter[quarter][:, t : t + count, :]
                 nc.vector.tensor_tensor(
                     summed[:, t : t + count, :],
                     bank[:, :, in_bank : in_bank + width],
-                    load[:, t : t + count, in_load : in_load + width],
+                    pos_here[:, :, in_quarter : in_quarter + width],
                     ADD,
                 )
             nc.scalar.activation(
@@ -232,7 +242,7 @@ def tile_picked_phpq_gelu_p_kernel(
                 GELU,
             )
             first = first + width
-        for rest in range(len(OUT_WIDTHS) - len(EARLY_PIECES_AT)):
+        for rest in OUT_WIDTHS[1:]:
             second_product()
 
         result = keep.tile([P, S], F32, name="result")

@@ -38,6 +38,7 @@ LATE_AT = 0
 SUMS_AT = LATE_AT + 4 * PACK * (H + LAST[0])
 SUM_BYTES = 4 * PACK * max(GELU_WIDTHS)
 W1_FIRST_AT = SUMS_AT + SUM_SLOTS * SUM_BYTES
+W2_PLANE_AT = W1_FIRST_AT + 4 * PACK * QUARTER
 
 
 def tile_picked_phpq_gelu_p_kernel(
@@ -94,7 +95,7 @@ def tile_picked_phpq_gelu_p_kernel(
 
         picked = [
             keep.tile([P, S], U32, name="picked0", align_bytes=64),
-            placed.tile([P, S], U32, name="picked1", align_bytes=64, offset=W1_FIRST_AT + 4 * PACK * QUARTER),
+            placed.tile([P, S], U32, name="picked1", align_bytes=64, offset=W2_PLANE_AT + N),
         ]
         w1_codes, w1_plane = {}, {}
 
@@ -133,6 +134,8 @@ def tile_picked_phpq_gelu_p_kernel(
         round_w1(nc.vector.tensor_copy, 0, 1, slice(SCALAR_SHARE_PASS0, P))
         for u in range(2):
             quantize_w1(0, u, 1)
+        w2_plane = placed.tile([P, N], U8, name="w2_plane", align_bytes=64, offset=W2_PLANE_AT)
+        nc.vector.memset(w2_plane[:].bitcast(I32), 0)
         gather_words(1)
 
         pos_last = [
@@ -142,8 +145,6 @@ def tile_picked_phpq_gelu_p_kernel(
         for u in range(2):
             nc.sync.dma_start(pos_last[u][:], pos_rows[:, 2 * u : 2 * u + 2, LAST[0] :])
 
-        w2_plane = keep.tile([P, N], U8, name="w2_plane", tag="grouped01", align_bytes=64)
-        nc.gpsimd.memset(w2_plane[:].bitcast(I32), 0)
         for q in range(P // QUADRANT):
             nc.sync.dma_start(
                 w2_plane[QUADRANT * q : QUADRANT * q + 4, :].bitcast(I32), w2_scales[0, 4 * q : 4 * q + 4, :].bitcast(I32)

@@ -26,19 +26,22 @@ QUADRANT = 32
 TABLE_HEAD = 768
 QUARTER = S // 4
 LEAD, MIDDLE, LAST = (0, QUARTER), (QUARTER, 2 * QUARTER), (3 * QUARTER, QUARTER)
+POS_WIDTHS = (384, 256, 256)
+POS_LAST = sum(POS_WIDTHS)
 SCALAR_SHARE_PASS0 = 48
 SCALAR_SHARE_PASS1 = 56
 GELU_WIDTHS = (128, 128, 128, 128, 128, 128, 128, 64, 64)
 SUM_SLOTS = 5
 OUT_WIDTHS = (256, 256, 256, 128, 128)
 OUT_BANKS = (2, 3, 4, 5, 6)
-EARLY_PIECE_AT = 512
+EARLY_PIECES_AT = (640, 896)
 SCALAR_PIECES = 2
 LATE_AT = 0
-SUMS_AT = LATE_AT + 4 * PACK * (H + LAST[0])
+SUMS_AT = LATE_AT + 4 * PACK * (H + POS_LAST)
 SUM_BYTES = 4 * PACK * max(GELU_WIDTHS)
 W1_FIRST_AT = SUMS_AT + SUM_SLOTS * SUM_BYTES
-W2_PLANE_AT = W1_FIRST_AT + 4 * PACK * QUARTER
+PAIR_BYTES = 4 * 2 * (S - POS_LAST)
+W2_PLANE_AT = W1_FIRST_AT + 2 * PAIR_BYTES
 
 
 def tile_picked_phpq_gelu_p_kernel(
@@ -73,7 +76,7 @@ def tile_picked_phpq_gelu_p_kernel(
         picked_scales = keep.tile([P, S], U8, name="picked_scales", align_bytes=64)
         nc.vector.tensor_copy(picked_scales[:], scale_table[:].indirect(lists[:]))
 
-        late = placed.tile([P, PACK * (H + LAST[0])], F32, name="late", align_bytes=64, offset=LATE_AT)
+        late = placed.tile([P, PACK * (H + POS_LAST)], F32, name="late", align_bytes=64, offset=LATE_AT)
         w1_raw = [w1_first[:], late[:, : PACK * H].rearrange("p (j c) -> p j c", j=PACK)]
 
         def move_scale_rows(z):
@@ -87,11 +90,13 @@ def tile_picked_phpq_gelu_p_kernel(
         nc.sync.dma_start(w1_raw[1], w1_rows[1])
         move_scale_rows(1)
         pos_rows = pos.rearrange("(p t) c -> p t c", t=PACK)
-        pos_quarter = []
-        for first in range(0, LAST[0], QUARTER):
-            load = late[:, PACK * (H + first) : PACK * (H + first + QUARTER)].rearrange("p (t c) -> p t c", t=PACK)
-            nc.sync.dma_start(load, pos_rows[:, :, first : first + QUARTER])
-            pos_quarter.append(load)
+        pos_loads = []
+        first = 0
+        for width in POS_WIDTHS:
+            load = late[:, PACK * (H + first) : PACK * (H + first + width)].rearrange("p (t c) -> p t c", t=PACK)
+            nc.sync.dma_start(load, pos_rows[:, :, first : first + width])
+            pos_loads.append((first, lambda t, count, load=load: load[:, t : t + count, :]))
+            first = first + width
 
         picked = [
             keep.tile([P, S], U32, name="picked0", align_bytes=64),
@@ -139,11 +144,14 @@ def tile_picked_phpq_gelu_p_kernel(
         gather_words(1)
 
         pos_last = [
-            placed.tile([P, 2, QUARTER], F32, name=f"pos_last{u}", align_bytes=64, offset=W1_FIRST_AT + u * 4 * 2 * QUARTER)
+            placed.tile(
+                [P, 2, S - POS_LAST], F32, name=f"pos_last{u}", align_bytes=64, offset=W1_FIRST_AT + u * PAIR_BYTES
+            )
             for u in range(2)
         ]
         for u in range(2):
-            nc.sync.dma_start(pos_last[u][:], pos_rows[:, 2 * u : 2 * u + 2, LAST[0] :])
+            nc.sync.dma_start(pos_last[u][:], pos_rows[:, 2 * u : 2 * u + 2, POS_LAST:])
+        pos_loads.append((POS_LAST, lambda t, count: pos_last[t // 2][:]))
 
         for q in range(P // QUADRANT):
             nc.sync.dma_start(
@@ -196,9 +204,8 @@ def tile_picked_phpq_gelu_p_kernel(
 
         def second_product():
             first, width = sum(OUT_WIDTHS[: len(pieces)]), OUT_WIDTHS[len(pieces)]
-            if pieces:
-                codes_at = W1_FIRST_AT + 4 * (first - OUT_WIDTHS[0])
-                h_codes = placed.tile([P, width], U32, name=f"h_codes{first}", align_bytes=64, offset=codes_at)
+            if len(pieces) == len(EARLY_PIECES_AT):
+                h_codes = placed.tile([P, width], U32, name=f"h_codes{first}", align_bytes=64, offset=W1_FIRST_AT)
             else:
                 h_codes = keep.tile([P, width], U32, name=f"h_codes{first}", align_bytes=64)
             h_plane = keep.tile([P, width], U8, name=f"h_plane{first}", align_bytes=64)
@@ -221,20 +228,20 @@ def tile_picked_phpq_gelu_p_kernel(
         for piece, width in enumerate(GELU_WIDTHS):
             if first == MIDDLE[0]:
                 multiply_last_stretch()
-            if first == EARLY_PIECE_AT:
+            if first in EARLY_PIECES_AT:
                 second_product()
             stretch = max(s for s in (LEAD, MIDDLE, LAST) if s[0] <= first)
             in_bank = first - stretch[0]
-            quarter, in_quarter = divmod(first, QUARTER)
+            load_first, rows_of = [entry for entry in pos_loads if entry[0] <= first][-1]
+            in_load = first - load_first
             summed = placed.tile(
                 [P, PACK, width], F32, name=f"summed{piece}", align_bytes=64, offset=SUMS_AT + piece % SUM_SLOTS * SUM_BYTES
             )
             for bank, t, count in held[stretch]:
-                pos_here = pos_last[t // 2][:] if stretch == LAST else pos_quarter[quarter][:, t : t + count, :]
                 nc.vector.tensor_tensor(
                     summed[:, t : t + count, :],
                     bank[:, :, in_bank : in_bank + width],
-                    pos_here[:, :, in_quarter : in_quarter + width],
+                    rows_of(t, count)[:, :, in_load : in_load + width],
                     ADD,
                 )
             nc.scalar.activation(
@@ -243,7 +250,7 @@ def tile_picked_phpq_gelu_p_kernel(
                 GELU,
             )
             first = first + width
-        for rest in OUT_WIDTHS[1:]:
+        for rest in OUT_WIDTHS[len(EARLY_PIECES_AT) :]:
             second_product()
 
         result = keep.tile([P, S], F32, name="result")

@@ -25,16 +25,16 @@ BLOCK = 8
 QUADRANT = 32
 TABLE_HEAD = 768
 QUARTER = S // 4
-LEAD, MIDDLE, LAST = (0, QUARTER), (QUARTER, 2 * QUARTER), (3 * QUARTER, QUARTER)
-POS_WIDTHS = (384, 256, 256)
+LEAD, SECOND, THIRD, LAST = [(q * QUARTER, QUARTER) for q in range(4)]
+POS_WIDTHS = (256, 320, 256)
 POS_LAST = sum(POS_WIDTHS)
 SCALAR_SHARE_PASS0 = 48
-SCALAR_SHARE_PASS1 = 56
-GELU_WIDTHS = (128, 128, 128, 128, 128, 128, 128, 64, 64)
+SCALAR_SHARES_PASS1 = (56, 72)
+GELU_WIDTHS = (128, 128, 128, 128, 64, 128, 64, 64, 128, 64)
 SUM_SLOTS = 5
 OUT_WIDTHS = (256, 256, 256, 128, 128)
 OUT_BANKS = (2, 3, 4, 5, 6)
-EARLY_PIECES_AT = (640, 896)
+EARLY_PIECES_AT = (704, 960)
 SCALAR_PIECES = 2
 LATE_AT = 0
 SUMS_AT = LATE_AT + 4 * PACK * (H + POS_LAST)
@@ -161,12 +161,12 @@ def tile_picked_phpq_gelu_p_kernel(
         nc.sync.dma_start(w2_codes[:].bitcast(I32), w2_words[0].bitcast(I32))
 
         for u in range(2):
-            round_w1(nc.scalar.copy, 1, u, slice(0, SCALAR_SHARE_PASS1))
-            round_w1(nc.vector.tensor_copy, 1, u, slice(SCALAR_SHARE_PASS1, P))
+            round_w1(nc.scalar.copy, 1, u, slice(0, SCALAR_SHARES_PASS1[u]))
+            round_w1(nc.vector.tensor_copy, 1, u, slice(SCALAR_SHARES_PASS1[u], P))
         for u in range(2):
             quantize_w1(1, u, 2)
 
-        def first_product(acc, z, t, stretch):
+        def first_product(acc, z, t, stretch, start, stop):
             first, width = stretch
             nc.tensor.matmul_mx(
                 out=acc,
@@ -174,21 +174,23 @@ def tile_picked_phpq_gelu_p_kernel(
                 lhsT_scale=w1_plane[z, t],
                 rhs=picked[z][:, first : first + width].bitcast(FP8X4),
                 rhs_scale=x_plane[z][:, first : first + width],
-                start=(z == 0),
-                stop=(z == PASSES - 1),
+                start=start,
+                stop=stop,
             )
 
-        held = {
-            stretch: [
-                (psum.tile([P, 1, stretch[1]], F32, name=f"bank{bank0 + t}", tag=f"bank{bank0 + t}"), t, 1)
-                for t in range(PACK)
+        held = {LEAD: [(psum.tile([P, 1, QUARTER], F32, name=f"bank{t}", tag=f"bank{t}"), t, 1) for t in range(PACK)]}
+        for stretch, bank0 in ((SECOND, 4), (THIRD, 6)):
+            held[stretch] = [
+                (psum.tile([P, 2, QUARTER], F32, name=f"bank{bank0 + u}", tag=f"bank{bank0 + u}"), 2 * u, 2)
+                for u in range(2)
             ]
-            for stretch, bank0 in ((LEAD, 0), (MIDDLE, PACK))
-        }
         for z in range(PASSES):
-            for stretch in (LEAD, MIDDLE):
+            for stretch in (LEAD, SECOND, THIRD):
                 for bank, t, count in held[stretch]:
-                    first_product(bank[:, 0, :], z, t, stretch)
+                    for e in range(count):
+                        first_product(
+                            bank[:, e, :], z, t + e, stretch, z == 0 and e == 0, z == PASSES - 1 and e == count - 1
+                        )
 
         def multiply_last_stretch():
             held[LAST] = [
@@ -197,7 +199,7 @@ def tile_picked_phpq_gelu_p_kernel(
             for bank, t, count in held[LAST]:
                 for e in range(count):
                     for z in range(PASSES):
-                        first_product(bank[:, e, :], z, t + e, LAST)
+                        first_product(bank[:, e, :], z, t + e, LAST, z == 0, z == PASSES - 1)
 
         hidden = keep.tile([P, PACK * S], BF16, name="hidden", align_bytes=64)
         pieces = []
@@ -226,11 +228,11 @@ def tile_picked_phpq_gelu_p_kernel(
 
         first = 0
         for piece, width in enumerate(GELU_WIDTHS):
-            if first == MIDDLE[0]:
+            if first == SECOND[0]:
                 multiply_last_stretch()
             if first in EARLY_PIECES_AT:
                 second_product()
-            stretch = max(s for s in (LEAD, MIDDLE, LAST) if s[0] <= first)
+            stretch = max(s for s in (LEAD, SECOND, THIRD, LAST) if s[0] <= first)
             in_bank = first - stretch[0]
             load_first, rows_of = [entry for entry in pos_loads if entry[0] <= first][-1]
             in_load = first - load_first

@@ -29,7 +29,7 @@ LEAD, SECOND, THIRD, LAST = [(q * QUARTER, QUARTER) for q in range(4)]
 POS_WIDTHS = (256, 320, 256)
 POS_LAST = sum(POS_WIDTHS)
 SCALAR_SHARE_PASS0 = 48
-SCALAR_SHARES_PASS1 = (56, 72)
+SCALAR_SHARES_PASS1 = (52, 44)
 GELU_WIDTHS = (128, 128, 128, 128, 64, 128, 64, 64, 128, 64)
 SUM_SLOTS = 5
 OUT_WIDTHS = (256, 256, 256, 128, 128)
@@ -163,8 +163,8 @@ def tile_picked_phpq_gelu_p_kernel(
         for u in range(2):
             round_w1(nc.scalar.copy, 1, u, slice(0, SCALAR_SHARES_PASS1[u]))
             round_w1(nc.vector.tensor_copy, 1, u, slice(SCALAR_SHARES_PASS1[u], P))
-        for u in range(2):
-            quantize_w1(1, u, 2)
+        quantize_w1(1, 0, 1)
+        quantize_w1(1, 1, 2)
 
         def first_product(acc, z, t, stretch, start, stop):
             first, width = stretch
@@ -247,8 +247,8 @@ def tile_picked_phpq_gelu_p_kernel(
                     ADD,
                 )
             nc.scalar.activation(
-                hidden[:, PACK * first : PACK * (first + width)].rearrange("p (c n t) -> p c t n", n=2, t=PACK),
-                summed[:].rearrange("p t (c n) -> p c t n", n=2),
+                hidden[:, PACK * first : PACK * (first + width)].rearrange("p (c n t) -> p c t n", n=4, t=PACK),
+                summed[:].rearrange("p t (c n) -> p c t n", n=4),
                 GELU,
             )
             first = first + width

@@ -63,6 +63,9 @@ def tile_picked_phpq_gelu_p_kernel(
         nc.vector.memset(scale_table[:].bitcast(I32), 0)
         for z in range(PASSES):
             nc.sync.dma_start(scale_table[4 * z : P : BLOCK, :].bitcast(I32), x_scales[z].bitcast(I32))
+        warm = keep.tile([P, 2], F32, name="warm")
+        nc.vector.memset(warm[:, 0:1], 0.0)
+        nc.scalar.activation(warm[:, 1:2], warm[:, 0:1], GELU)
         x_plane = [keep.tile([P, S], U8, name=f"x_plane{z}", align_bytes=64) for z in range(PASSES)]
         for z in range(PASSES):
             nc.vector.memset(x_plane[z][:].bitcast(I32), 0)

from contextlib import ExitStack

import concourse.mybir as mybir

K, T, S, H, N = 1024, 2048, 1024, 512, 128
FLOPS = 2 * K * H * S + 2 * H * N * S

F32 = mybir.dt.float32
BF16 = mybir.dt.bfloat16
I32 = mybir.dt.int32
U32 = mybir.dt.uint32
U16 = mybir.dt.uint16
U8 = mybir.dt.uint8
FP8X4 = mybir.dt.float8_e4m3fn_x4
FP4X4 = mybir.dt.float4_e2m1fn_x4
GELU = mybir.ActivationFunctionType.Gelu_apprx_tanh
ADD = mybir.AluOpType.add

P = 128
PACK = 4
K_PASS = P * PACK
PASSES = K // K_PASS
GROUP = 16
BLOCK = 8
QUADRANT = 32
TABLE_HEAD = 768
QUARTER = S // 4
LEAD, SECOND, THIRD, LAST = [(q * QUARTER, QUARTER) for q in range(4)]
POS_WIDTHS = (256, 320, 256)
POS_LAST = sum(POS_WIDTHS)
SCALAR_SHARE_PASS0 = 48
SCALAR_SHARES_PASS1 = (52, 44)
GELU_WIDTHS = (128, 128, 128, 128, 64, 128, 64, 64, 128, 64)
SUM_SLOTS = 5
OUT_WIDTHS = (256, 256, 256, 128, 128)
OUT_BANKS = (2, 3, 4, 5, 6)
EARLY_PIECES_AT = (704, 960)
SCALAR_PIECES = 2
LATE_AT = 0
SUMS_AT = LATE_AT + 4 * PACK * (H + POS_LAST)
SUM_BYTES = 4 * PACK * max(GELU_WIDTHS)
W1_FIRST_AT = SUMS_AT + SUM_SLOTS * SUM_BYTES
PAIR_BYTES = 4 * 2 * (S - POS_LAST)
W2_PLANE_AT = W1_FIRST_AT + 2 * PAIR_BYTES


def tile_picked_phpq_gelu_p_kernel(
    tc, x_words, x_scales, w1, w2_words, w2_scales, pos, offs, out
):
    nc = tc.nc
    with ExitStack() as ctx:
        keep = ctx.enter_context(tc.tile_pool(name="keep", bufs=1))
        placed = ctx.enter_context(tc.tile_pool(name="placed", bufs=1))
        psum = ctx.enter_context(tc.psum_pool(name="psum", bufs=1))

        word_table = [keep.tile([P, T], I32, name=f"word_table{z}", align_bytes=64) for z in range(PASSES)]
        table_rows = [x_words[z].rearrange("p c r -> p (c r)").bitcast(I32) for z in range(PASSES)]
        nc.sync.dma_start(word_table[0][:, :TABLE_HEAD], table_rows[0][:, :TABLE_HEAD])
        lists = keep.tile([P, S // GROUP], U16, name="lists")
        nc.sync.dma_start(lists[:], offs)

        scale_table = placed.tile([P, T], U8, name="scale_table", align_bytes=64, offset=LATE_AT)
        nc.vector.memset(scale_table[:].bitcast(I32), 0)
        for z in range(PASSES):
            nc.sync.dma_start(scale_table[4 * z : P : BLOCK, :].bitcast(I32), x_scales[z].bitcast(I32))
        warm = keep.tile([P, 2], F32, name="warm")
        nc.vector.memset(warm[:, 0:1], 0.0)
        nc.scalar.activation(warm[:, 1:2], warm[:, 0:1], GELU)
        x_plane = [keep.tile([P, S], U8, name=f"x_plane{z}", align_bytes=64) for z in range(PASSES)]
        for z in range(PASSES):
            nc.vector.memset(x_plane[z][:].bitcast(I32), 0)

        w1_rows = [w1[z * K_PASS : (z + 1) * K_PASS, :].rearrange("(p j) c -> p j c", j=PACK) for z in range(PASSES)]
        w1_first = placed.tile([P, PACK, H], F32, name="w1_first", align_bytes=64, offset=W1_FIRST_AT)
        nc.sync.dma_start(word_table[0][:, TABLE_HEAD:], table_rows[0][:, TABLE_HEAD:])
        nc.sync.dma_start(w1_first[:], w1_rows[0])
        nc.sync.dma_start(word_table[1][:], table_rows[1])

        picked_scales = keep.tile([P, S], U8, name="picked_scales", align_bytes=64)
        nc.vector.tensor_copy(picked_scales[:], scale_table[:].indirect(lists[:]))

        late = placed.tile([P, PACK * (H + POS_LAST)], F32, name="late", align_bytes=64, offset=LATE_AT)
        w1_raw = [w1_first[:], late[:, : PACK * H].rearrange("p (j c) -> p j c", j=PACK)]

        def move_scale_rows(z):
            for r in range(QUADRANT // BLOCK):
                nc.sync.dma_start(
                    x_plane[z][r:P:QUADRANT, :].bitcast(I32),
                    picked_scales[BLOCK * r + 4 * z : P : QUADRANT, :].bitcast(I32),
                )

        move_scale_rows(0)
        nc.sync.dma_start(w1_raw[1], w1_rows[1])
        move_scale_rows(1)
        pos_rows = pos.rearrange("(p t) c -> p t c", t=PACK)
        pos_loads = []
        first = 0
        for width in POS_WIDTHS:
            load = late[:, PACK * (H + first) : PACK * (H + first + width)].rearrange("p (t c) -> p t c", t=PACK)
            nc.sync.dma_start(load, pos_rows[:, :, first : first + width])
            pos_loads.append((first, lambda t, count, load=load: load[:, t : t + count, :]))
            first = first + width

        picked = [
            keep.tile([P, S], U32, name="picked0", align_bytes=64),
            placed.tile([P, S], U32, name="picked1", align_bytes=64, offset=W2_PLANE_AT + N),
        ]
        w1_codes, w1_plane = {}, {}

        def gather_words(z):
            nc.vector.tensor_copy(picked[z][:], word_table[z][:].bitcast(U32).indirect(lists[:]))

        grouped = {
            (z, u): keep.tile([P, 2 * H], BF16, name=f"w1_grouped{z}{u}", tag=f"grouped{z}{u}", align_bytes=64)
            for z in range(PASSES)
            for u in range(2)
        }

        def round_w1(engine_copy, z, u, columns):
            engine_copy(
                grouped[z, u][:].rearrange("p (e m j) -> p m j e", e=2, j=PACK)[:, columns],
                w1_raw[z].rearrange("p j (m u e) -> p u m j e", u=2, e=2)[:, u, columns],
            )

        def quantize_w1(z, u, calls):
            codes = keep.tile([P, 2 * P], U32, name=f"w1_codes{z}{u}", align_bytes=64)
            plane = keep.tile([P, 2 * P], U8, name=f"w1_plane{z}{u}", align_bytes=64)
            step = 2 * P // calls
            for c in range(0, 2 * P, step):
                nc.vector.quantize_mx(
                    out=codes[:, c : c + step].bitcast(FP8X4),
                    scales=plane[:, c : c + step],
                    in_=grouped[z, u][:, PACK * c : PACK * (c + step)],
                )
            for e in range(2):
                w1_codes[z, 2 * u + e] = codes[:, e * P : (e + 1) * P]
                w1_plane[z, 2 * u + e] = plane[:, e * P : (e + 1) * P]

        gather_words(0)
        round_w1(nc.scalar.copy, 0, 0, slice(0, P))
        round_w1(nc.scalar.copy, 0, 1, slice(0, SCALAR_SHARE_PASS0))
        round_w1(nc.vector.tensor_copy, 0, 1, slice(SCALAR_SHARE_PASS0, P))
        for u in range(2):
            quantize_w1(0, u, 1)
        w2_plane = placed.tile([P, N], U8, name="w2_plane", align_bytes=64, offset=W2_PLANE_AT)
        nc.vector.memset(w2_plane[:].bitcast(I32), 0)
        gather_words(1)

        pos_last = [
            placed.tile(
                [P, 2, S - POS_LAST], F32, name=f"pos_last{u}", align_bytes=64, offset=W1_FIRST_AT + u * PAIR_BYTES
            )
            for u in range(2)
        ]
        for u in range(2):
            nc.sync.dma_start(pos_last[u][:], pos_rows[:, 2 * u : 2 * u + 2, POS_LAST:])
        pos_loads.append((POS_LAST, lambda t, count: pos_last[t // 2][:]))

        for q in range(P // QUADRANT):
            nc.sync.dma_start(
                w2_plane[QUADRANT * q : QUADRANT * q + 4, :].bitcast(I32), w2_scales[0, 4 * q : 4 * q + 4, :].bitcast(I32)
            )
        w2_codes = keep.tile([P, 2 * N], U8, name="w2_codes", tag="grouped00", align_bytes=64)
        nc.sync.dma_start(w2_codes[:].bitcast(I32), w2_words[0].bitcast(I32))

        for u in range(2):
            round_w1(nc.scalar.copy, 1, u, slice(0, SCALAR_SHARES_PASS1[u]))
            round_w1(nc.vector.tensor_copy, 1, u, slice(SCALAR_SHARES_PASS1[u], P))
        quantize_w1(1, 0, 1)
        quantize_w1(1, 1, 2)

        def first_product(acc, z, t, stretch, start, stop):
            first, width = stretch
            nc.tensor.matmul_mx(
                out=acc,
                lhsT=w1_codes[z, t].bitcast(FP8X4),
                lhsT_scale=w1_plane[z, t],
                rhs=picked[z][:, first : first + width].bitcast(FP8X4),
                rhs_scale=x_plane[z][:, first : first + width],
                start=start,
                stop=stop,
            )

        held = {LEAD: [(psum.tile([P, 1, QUARTER], F32, name=f"bank{t}", tag=f"bank{t}"), t, 1) for t in range(PACK)]}
        for stretch, bank0 in ((SECOND, 4), (THIRD, 6)):
            held[stretch] = [
                (psum.tile([P, 2, QUARTER], F32, name=f"bank{bank0 + u}", tag=f"bank{bank0 + u}"), 2 * u, 2)
                for u in range(2)
            ]
        for z in range(PASSES):
            for stretch in (LEAD, SECOND, THIRD):
                for bank, t, count in held[stretch]:
                    for e in range(count):
                        first_product(
                            bank[:, e, :], z, t + e, stretch, z == 0 and e == 0, z == PASSES - 1 and e == count - 1
                        )

        def multiply_last_stretch():
            held[LAST] = [
                (psum.tile([P, 2, QUARTER], F32, name=f"pair{u}", tag=f"bank{u}"), 2 * u, 2) for u in range(2)
            ]
            for bank, t, count in held[LAST]:
                for e in range(count):
                    for z in range(PASSES):
                        first_product(bank[:, e, :], z, t + e, LAST, z == 0, z == PASSES - 1)

        hidden = keep.tile([P, PACK * S], BF16, name="hidden", align_bytes=64)
        pieces = []

        def second_product():
            first, width = sum(OUT_WIDTHS[: len(pieces)]), OUT_WIDTHS[len(pieces)]
            if len(pieces) == len(EARLY_PIECES_AT):
                h_codes = placed.tile([P, width], U32, name=f"h_codes{first}", align_bytes=64, offset=W1_FIRST_AT)
            else:
                h_codes = keep.tile([P, width], U32, name=f"h_codes{first}", align_bytes=64)
            h_plane = keep.tile([P, width], U8, name=f"h_plane{first}", align_bytes=64)
            nc.vector.quantize_mx(
                out=h_codes[:].bitcast(FP8X4), scales=h_plane[:], in_=hidden[:, PACK * first : PACK * (first + width)]
            )
            acc = psum.tile([P, width], F32, name="acc", tag=f"bank{OUT_BANKS[len(pieces)]}")
            nc.tensor.matmul_mx(
                out=acc[:],
                lhsT=w2_codes[:].bitcast(FP4X4),
                lhsT_scale=w2_plane[:],
                rhs=h_codes[:].bitcast(FP8X4),
                rhs_scale=h_plane[:],
                start=True,
                stop=True,
            )
            pieces.append((acc, slice(first, first + width)))

        first = 0
        for piece, width in enumerate(GELU_WIDTHS):
            if first == SECOND[0]:
                multiply_last_stretch()
            if first in EARLY_PIECES_AT:
                second_product()
            stretch = max(s for s in (LEAD, SECOND, THIRD, LAST) if s[0] <= first)
            in_bank = first - stretch[0]
            load_first, rows_of = [entry for entry in pos_loads if entry[0] <= first][-1]
            in_load = first - load_first
            summed = placed.tile(
                [P, PACK, width], F32, name=f"summed{piece}", align_bytes=64, offset=SUMS_AT + piece % SUM_SLOTS * SUM_BYTES
            )
            for bank, t, count in held[stretch]:
                nc.vector.tensor_tensor(
                    summed[:, t : t + count, :],
                    bank[:, :, in_bank : in_bank + width],
                    rows_of(t, count)[:, :, in_load : in_load + width],
                    ADD,
                )
            nc.scalar.activation(
                hidden[:, PACK * first : PACK * (first + width)].rearrange("p (c n t) -> p c t n", n=4, t=PACK),
                summed[:].rearrange("p t (c n) -> p c t n", n=4),
                GELU,
            )
            first = first + width
        for rest in OUT_WIDTHS[len(EARLY_PIECES_AT) :]:
            second_product()

        result = keep.tile([P, S], F32, name="result")
        for piece, (acc, vectors) in enumerate(pieces):
            engine_copy = nc.scalar.copy if piece < SCALAR_PIECES else nc.vector.tensor_copy
            engine_copy(result[:, vectors], acc[:])
            nc.sync.dma_start(out[:, vectors], result[:, vectors])
